import numpy as np
import ml_dtypes


def mxq(x, axis, fmt="e4m3"):
    dtype, down = {"e4m3": (ml_dtypes.float8_e4m3fn, 7), "e5m2": (ml_dtypes.float8_e5m2, 14)}[fmt]
    v = np.moveaxis(np.asarray(x, np.float32).astype(ml_dtypes.bfloat16).astype(np.float64), axis, -1)
    blocks = v.reshape(v.shape[:-1] + (-1, 32))
    amax = np.abs(blocks).max(-1, keepdims=True)
    byte = np.maximum(np.where(amax > 0, np.frexp(amax)[1] - 1 + 127, 0) - down, 1)
    scale = np.exp2(byte - 127.0)
    codes = (blocks / scale).astype(np.float32).astype(dtype).astype(np.float64)
    return np.moveaxis((codes * scale).reshape(v.shape), -1, axis)


WIDE = False


def mx_kscale(k):
    if not WIDE:
        return np.ones(k)
    levels = np.array([10, -10, 5, -5, 0])
    if k % 512:
        return np.exp2(np.random.permutation(np.resize(levels, k // 32))).repeat(32)
    a = np.empty((k // 512, 16))
    for p in range(k // 512):
        a[p, :8] = np.random.permutation(np.resize(levels, 8))
        for g in range(8):
            far = levels[np.abs(levels - a[p, g]) >= 10]
            a[p, g + 8] = far[np.random.randint(len(far))]
    return np.exp2(a.ravel()).repeat(32)


BF16 = ml_dtypes.bfloat16


def bf(x):
    return np.asarray(x, np.float32).astype(BF16)


def f64(x):
    return np.asarray(x).astype(np.float64)


E2M1 = np.array([0.0, 0.5, 1.0, 1.5, 2.0, 3.0, 4.0, 6.0, -0.0, -0.5, -1.0, -1.5, -2.0, -3.0, -4.0, -6.0])


def pack_weight(w, fmt):
    k, n = w.shape
    w = f64(bf(w)).reshape(k // 32, 32, n)
    amax = np.abs(w).max(1)
    if fmt == "e4m3":
        byte = np.frexp(amax)[1] - 1 + 127 - 7
    else:
        mant, ex = np.frexp(amax / 6.0)
        byte = np.where(mant > 0.5, ex, ex - 1) + 127
    byte = np.clip(np.where(amax > 0, byte, 1), 1, 254)
    scaled = (w * np.exp2(127.0 - byte)[:, None, :]).reshape(k, n).astype(np.float32)
    by_word = np.ascontiguousarray(scaled.reshape(k // 512, 128, 4, n).transpose(0, 1, 3, 2))
    if fmt == "e4m3":
        words = by_word.astype(ml_dtypes.float8_e4m3fn).view(np.uint8)
    else:
        c = by_word.astype(ml_dtypes.float4_e2m1fn).view(np.uint8) & 0xF
        words = c[..., 0::2] | (c[..., 1::2] << 4)
    return np.ascontiguousarray(words), np.ascontiguousarray(byte.astype(np.uint8).reshape(k // 512, 16, n))


def unpack_weight(words, scales, fmt):
    g, p, n, _ = words.shape
    if fmt == "e4m3":
        vals = np.ascontiguousarray(words).view(ml_dtypes.float8_e4m3fn).astype(np.float64)
    else:
        nib = np.empty((g, p, n, 4), np.uint8)
        nib[..., 0::2] = words & 0xF
        nib[..., 1::2] = words >> 4
        vals = E2M1[nib]
    vals = vals * np.repeat(np.exp2(scales.astype(np.float64) - 127.0), 8, axis=1)[..., None]
    return vals.transpose(0, 1, 3, 2).reshape(g * 512, n)
def pack4(w):
    words, scales = pack_weight(w, "e2m1")
    return words.reshape(words.shape[0], 128, -1), scales


def unpack4(words, scales):
    return unpack_weight(words.reshape(words.shape[0], 128, -1, 2), scales, "e2m1")


P, T, D, H, S = 8, 2048, 1024, 1024, 1536


def setup_inputs():
    s = mx_kscale(D)
    u = mx_kscale(T)
    x = np.random.standard_normal((T, D)) * s * u[:, None]
    w = np.random.standard_normal((D, H)) / np.sqrt(D) / s[:, None]
    lhuc = np.random.standard_normal((P, H))
    err = np.random.standard_normal((T, S)) / np.sqrt(T) / u[:, None]
    err_words, err_scales = pack4(err)
    return {"x": bf(x),
            "w": bf(w),
            "lhuc": bf(lhuc),
            "err_words": err_words,
            "err_scales": err_scales}


def reference(x, w, lhuc, err_words, err_scales):
    z = mxq(f64(x), 1, "e4m3") @ mxq(f64(w), 0, "e4m3")
    amp = 2.0 / (1.0 + np.exp(-f64(lhuc)))
    h = np.maximum(z, 0.0).reshape(P, T // P, H) * amp[:, None, :]
    h = h.reshape(T, H)
    e = unpack4(err_words, err_scales)
    return mxq(h, 0, "e4m3").T @ e

@@ -1,0 +1,382 @@
+from contextlib import ExitStack
+
+from concourse.masks import make_identity
+import concourse.mybir as mybir
+
+F32 = mybir.dt.float32
+BF16 = mybir.dt.bfloat16
+I32 = mybir.dt.int32
+U32 = mybir.dt.uint32
+U8 = mybir.dt.uint8
+FP8X4 = mybir.dt.float8_e4m3fn_x4
+FP4X4 = mybir.dt.float4_e2m1fn_x4
+ALU = mybir.AluOpType
+ACT = mybir.ActivationFunctionType
+
+T, D, H, S, SPK = 2048, 1024, 1024, 1536, 8
+P = 128
+G = T // 512
+Q = D // 512
+NH = H // P
+NS = S // 512
+WC = 256
+
+FLOPS = 2 * T * D * H + 2 * T * H * S
+BYTES = 2 * T * D + 2 * D * H + 2 * SPK * H + T * S // 2 + T * S // 32 + 4 * H * S
+
+
+def tile_lhuc_senone_gradient_s13_kernel(tc, x, w, lhuc, err_words, err_scales, out):
+    nc = tc.nc
+    with ExitStack() as ctx:
+        keep = ctx.enter_context(tc.tile_pool(name="keep", bufs=1))
+        work = ctx.enter_context(tc.tile_pool(name="work", bufs=4))
+        psum = ctx.enter_context(tc.psum_pool(name="psum", bufs=1))
+
+        ident = keep.tile([P, P], F32, name="ident")
+        identb = keep.tile([P, P], BF16, name="identb")
+        lrow = keep.tile([P, 512], BF16, name="lrow", align_bytes=64)
+        lcol = keep.tile([P, 4, SPK], BF16, name="lcol", align_bytes=64)
+        lrep = keep.tile([P, 2, G, 2, 2, 64], BF16, name="lrep", align_bytes=64)
+        dummy = keep.tile([P, 1], F32, name="dummy")
+        xraw = [keep.tile([P, 4, D], BF16, name="xraw%d" % g) for g in range(G)]
+        xcod = [keep.tile([P, 4, Q * P], U32, name="xcod%d" % g, align_bytes=64) for g in range(G)]
+        xsca = [keep.tile([P, 4, Q * P], U8, name="xsca%d" % g, align_bytes=64) for g in range(G)]
+        wraw = [[keep.tile([P, 4, WC], BF16, name="wraw%d_%d" % (c, q)) for q in range(Q)] for c in range(H // WC)]
+        wcod = [[keep.tile([P, WC], U32, name="wcod%d_%d" % (c, q), align_bytes=64) for q in range(Q)] for c in range(H // WC)]
+        wsca = [[keep.tile([P, WC], U8, name="wsca%d_%d" % (c, q), align_bytes=64) for q in range(Q)] for c in range(H // WC)]
+        lraw = [keep.tile([P, G, 512], BF16, name="lraw%d" % c) for c in range(2)]
+        amp = [keep.tile([P, G, 256], F32, name="amp%d" % c) for c in range(4)]
+        hcod = [keep.tile([P, G, P], U32, name="hcod%d" % h, align_bytes=64) for h in range(NH)]
+        hsca = [keep.tile([P, G, P], U8, name="hsca%d" % h, align_bytes=64) for h in range(NH)]
+        ewor = [keep.tile([P, 2 * S], U8, name="ewor%d" % g, align_bytes=64) for g in range(G)]
+        esca = keep.tile([P, G, S], U8, name="esca", align_bytes=64)
+
+        def bank(i):
+            b = psum.tile([P, 512], F32, name="bank%d" % i, tag="bank%d" % i)
+            return b
+
+        xbanks = [0, 1, 2, 3]
+        zbanks = [4, 5, 6]
+        obanks = [7, 1, 0, 3, 2]
+        count = {"z": 0, "o": 0}
+
+        def load_x(g, a, b):
+            nc.sync.dma_start(out=xraw[g][:, a:b, :], in_=x[512 * g : 512 * (g + 1), :].rearrange("(m t) k -> m t k", t=4)[:, a:b, :])
+
+        def load_w(c):
+            for q in range(Q):
+                nc.sync.dma_start(
+                    out=wraw[c][q][:],
+                    in_=w[512 * q : 512 * (q + 1), WC * c : WC * (c + 1)].rearrange("(p j) n -> p j n", j=4),
+                )
+
+        def load_lhuc(c, lo, hi):
+            rows = lhuc.rearrange("(g s) n -> s g n", s=2)
+            for s in range(2):
+                nc.sync.dma_start(
+                    out=lraw[c][64 * s : 64 * (s + 1), lo:hi, :],
+                    in_=rows[s, lo:hi, 512 * c : 512 * (c + 1)].partition_broadcast(64),
+                )
+
+        def load_esca():
+            for k in range(4):
+                nc.sync.dma_start(
+                    out=esca[32 * k : 32 * k + 4, :, :].bitcast(I32),
+                    in_=err_scales[:, 4 * k : 4 * (k + 1), :].rearrange("g r n -> r g n").bitcast(I32),
+                )
+
+        def load_ewor(g):
+            nc.sync.dma_start(out=ewor[g][:].bitcast(I32), in_=err_words[g].bitcast(I32))
+
+        xgrp = {}
+        xord = {}
+
+        def xorder(g, t, eng):
+            xo = work.tile([P, 512], F32, name="xo", tag="xo", bufs=6)
+            dst = xo[:].rearrange("p (q u m) -> p q u m", q=Q, u=2)
+            src = xraw[g][:, t, :].bitcast(F32).rearrange("p (q m u) -> p q u m", q=Q, u=2)
+            if eng == "s":
+                nc.scalar.copy(out=dst, in_=src)
+            else:
+                nc.vector.tensor_copy(out=dst, in_=src)
+            xord[g, t] = xo
+
+        def trans(g, t):
+            b = bank(xbanks[t])
+            words = xraw[g][:, t, :].bitcast(F32)
+            for q in range(Q):
+                for u in range(2):
+                    j = 2 * q + u
+                    if (g, t) in xord:
+                        cols = xord[g, t][:, P * j : P * (j + 1)]
+                    else:
+                        cols = words[:, 256 * q + u : 256 * (q + 1) : 2]
+                    nc.tensor.transpose(b[:, P * j : P * (j + 1)], cols, ident[:])
+            xg = work.tile([P, Q, P, 4], BF16, name="xg", tag="xg", align_bytes=64)
+            nc.scalar.copy(
+                out=xg[:].rearrange("p q m t -> p (q m t)").bitcast(F32),
+                in_=b[:].rearrange("p (q u m) -> p q m u", q=Q, u=2),
+            )
+            xgrp[g, t] = xg
+
+        def xquant(g, t):
+            nc.vector.quantize_mx(
+                out=xcod[g][:, t, :].bitcast(FP8X4),
+                scales=xsca[g][:, t, :],
+                in_=xgrp[g, t][:].rearrange("p q m t -> p (q m t)"),
+            )
+
+        wgrp = {}
+
+        def winter(h, q, eng, n=1):
+            c, off = divmod(P * h, WC)
+            wg = work.tile([P, P * n, 4], BF16, name="wg", tag="wg", align_bytes=64)
+            src = wraw[c][q][:, :, off : off + P * n].rearrange("p j n -> p n j")
+            if eng == "s":
+                nc.scalar.copy(out=wg[:], in_=src)
+            else:
+                nc.vector.tensor_copy(out=wg[:], in_=src)
+            wgrp[h, q] = wg
+
+        def wquant(h, q, n=1):
+            c, off = divmod(P * h, WC)
+            nc.vector.quantize_mx(
+                out=wcod[c][q][:, off : off + P * n].bitcast(FP8X4),
+                scales=wsca[c][q][:, off : off + P * n],
+                in_=wgrp[h, q][:].rearrange("p n j -> p (n j)"),
+            )
+
+        def lhuc_turn():
+            b = psum.tile([P, 4, P], BF16, name="bank5l", tag="bank5")
+            for h in range(4):
+                nc.tensor.transpose(b[:, h, :], lrow[:, P * h : P * (h + 1)], identb[:])
+            nc.vector.tensor_copy(out=lcol[:], in_=b[:, :, 0:SPK])
+
+        def lhuc_repeat(a, g, eng):
+            src = lcol[:, 2 * a : 2 * (a + 1), 2 * g : 2 * (g + 1)].unsqueeze(3).to_broadcast([P, 2, 2, 64])
+            if eng == "s":
+                nc.scalar.copy(out=lrep[:, a, g, :, :, :], in_=src)
+            else:
+                nc.vector.tensor_copy(out=lrep[:, a, g, :, :, :], in_=src)
+
+        def lhuc_spread(a, lo, hi, i):
+            b = psum.tile([P, G, 256], BF16, name="bank%dl" % i, tag="bank%d" % i)
+            for g in range(lo, hi):
+                for h in range(2):
+                    nc.tensor.transpose(
+                        b[:, g, P * h : P * (h + 1)], lrep[:, a, g, h, :, :].rearrange("p s r -> p (s r)"), identb[:]
+                    )
+            nc.scalar.activation(out=amp[a][:, lo:hi, :], in_=b[:, lo:hi, :], func=ACT.Sigmoid)
+
+        def sigm(c, lo, hi):
+            nc.scalar.activation(out=amp[c][:, lo:hi, :], in_=lraw[c // 2][:, lo:hi, 256 * (c % 2) : 256 * (c % 2 + 1)], func=ACT.Sigmoid)
+
+        zb = {}
+        hgrp = {}
+
+        def s1(g, h):
+            z = bank(zbanks[count["z"] % len(zbanks)])
+            count["z"] += 1
+            c, off = divmod(P * h, WC)
+            for t in range(4):
+                for q in range(Q):
+                    nc.tensor.matmul_mx(
+                        out=z[:, P * t : P * (t + 1)],
+                        lhsT=xcod[g][:, t, P * q : P * (q + 1)].bitcast(FP8X4),
+                        lhsT_scale=xsca[g][:, t, P * q : P * (q + 1)],
+                        rhs=wcod[c][q][:, off : off + P].bitcast(FP8X4),
+                        rhs_scale=wsca[c][q][:, off : off + P],
+                        start=(q == 0),
+                        stop=(q == Q - 1),
+                    )
+            zb[g, h] = z
+
+        def hevict(g, h):
+            c, off = divmod(P * h, 256)
+            hg = work.tile([P, P, 4], BF16, name="hg", tag="hg", align_bytes=64)
+            nc.vector.scalar_tensor_tensor(
+                out=hg[:],
+                in0=zb[g, h][:].rearrange("p (t n) -> p n t", t=4),
+                scalar=0.0,
+                in1=amp[c][:, g, off : off + P].unsqueeze(2).to_broadcast([P, P, 4]),
+                op0=ALU.max,
+                op1=ALU.mult,
+            )
+            hgrp[g, h] = hg
+
+        def hquant(g, h):
+            nc.vector.quantize_mx(
+                out=hcod[h][:, g, :].bitcast(FP8X4),
+                scales=hsca[h][:, g, :],
+                in_=hgrp[g, h][:].rearrange("p n t -> p (n t)"),
+            )
+
+        pend = []
+
+        def s1h(g, h):
+            s1(g, h)
+            hevict(g, h)
+            if pend:
+                hquant(*pend.pop())
+            pend.append((g, h))
+
+        def flush():
+            if pend:
+                hquant(*pend.pop())
+
+        ob = {}
+        og = {}
+
+        def s2(h, n, groups):
+            if groups[0] == 0:
+                ob[h, n] = bank(obanks[count["o"] % len(obanks)])
+                count["o"] += 1
+            for g in groups:
+                nc.tensor.matmul_mx(
+                    out=ob[h, n][:],
+                    lhsT=hcod[h][:, g, :].bitcast(FP8X4),
+                    lhsT_scale=hsca[h][:, g, :],
+                    rhs=ewor[g][:, 1024 * n : 1024 * (n + 1)].bitcast(FP4X4),
+                    rhs_scale=esca[:, g, 512 * n : 512 * (n + 1)],
+                    start=(g == 0),
+                    stop=(g == G - 1),
+                )
+
+        def oevict(h, n, eng, lo=0, hi=512):
+            if h not in og:
+                og[h] = work.tile([P, S], F32, name="og", tag="og", bufs=3)
+            dst = og[h][:, 512 * n + lo : 512 * n + hi]
+            src = ob[h, n][:, lo:hi]
+            if eng == "s":
+                nc.scalar.activation(out=dst, in_=src, func=ACT.Copy, scale=2.0)
+            else:
+                nc.vector.tensor_scalar(out=dst, in0=src, scalar1=2.0, scalar2=None, op0=ALU.mult)
+
+        def store(h, lo, hi):
+            nc.sync.dma_start(out=out[P * h : P * (h + 1), lo:hi], in_=og[h][:, lo:hi])
+
+        with tc.manual_schedule():
+            nc.vector.memset(dummy[:], 0.0)
+            nc.vector.memset(lrow[:], 0.0)
+            nc.scalar.dma_start(out=lrow[0:SPK, :], in_=lhuc[:, 0:512])
+            nc.scalar.activation(out=dummy[:], in_=dummy[:], func=ACT.Sigmoid)
+            make_identity(nc, ident[:])
+            make_identity(nc, identb[:])
+            nc.vector.memset(esca[:].rearrange("p g n -> p (g n)").bitcast(I32), 0)
+            load_x(0, 0, 1)
+            load_x(0, 1, 2)
+            load_x(0, 2, 3)
+            load_x(0, 3, 4)
+            load_w(0)
+            load_x(1, 0, 2)
+            load_x(1, 2, 4)
+            load_x(2, 0, 4)
+            load_x(3, 0, 4)
+            load_w(1)
+            load_esca()
+            for g in range(G):
+                load_ewor(g)
+            load_w(2)
+            load_w(3)
+            load_lhuc(1, 0, 4)
+
+            trans(0, 0)
+            trans(0, 1)
+            lhuc_turn()
+            lhuc_repeat(0, 0, "v")
+            trans(0, 2)
+            trans(0, 3)
+            xquant(0, 0)
+            xquant(0, 1)
+            winter(0, 0, "v")
+            winter(0, 1, "v")
+            xquant(0, 2)
+            wquant(0, 0)
+            wquant(0, 1)
+            xquant(0, 3)
+            lhuc_spread(0, 0, 1, 7)
+            winter(1, 0, "s")
+            winter(1, 1, "v")
+            lhuc_repeat(0, 1, "v")
+            wquant(1, 1)
+            wquant(1, 0)
+            lhuc_repeat(0, 2, "v")
+            lhuc_repeat(0, 3, "v")
+            s1h(0, 0)
+            trans(1, 0)
+            xquant(1, 0)
+            trans(1, 1)
+            xquant(1, 1)
+            xorder(2, 0, "v")
+            trans(1, 2)
+            xquant(1, 2)
+            xorder(2, 1, "v")
+            trans(1, 3)
+            xquant(1, 3)
+            xorder(2, 2, "v")
+            xorder(2, 3, "v")
+            lhuc_spread(0, 1, 4, 6)
+            s1h(0, 1)
+            for t in range(4):
+                trans(2, t)
+                xquant(2, t)
+                if t % 2:
+                    xorder(3, t, "v")
+            xorder(3, 0, "s")
+            s1h(1, 0)
+            s1h(1, 1)
+            for t in (1, 0, 3, 2):
+                trans(3, t)
+                xquant(3, t)
+            s1h(2, 0)
+            winter(2, 0, "s")
+            s1h(2, 1)
+            for g in (0, 1):
+                for n in range(NS):
+                    s2(0, n, [g])
+            winter(2, 1, "s")
+            for g in range(G):
+                lhuc_repeat(1, g, "s")
+            wquant(2, 0)
+            wquant(2, 1)
+            s1h(3, 0)
+            s1h(3, 1)
+            flush()
+            lhuc_spread(1, 0, 4, 3)
+            winter(3, 0, "s")
+            winter(3, 1, "v")
+            wquant(3, 0)
+            wquant(3, 1)
+            for h in range(NH):
+                z = h + 2
+                if z < NH:
+                    s1h(0, z)
+                if z == 3:
+                    winter(4, 0, "s", 2)
+                    winter(4, 1, "s", 2)
+                    sigm(2, 0, 4)
+                    wquant(4, 0, 2)
+                    wquant(4, 1, 2)
+                if z == 5:
+                    sigm(3, 0, 4)
+                    winter(6, 0, "s", 2)
+                    winter(6, 1, "s", 2)
+                    wquant(6, 0, 2)
+                    wquant(6, 1, 2)
+                for n in range(NS):
+                    s2(h, n, [2, 3] if h == 0 else [0, 1, 2, 3])
+                    if h < NH - 1:
+                        oevict(h, n, "s")
+                    elif n < NS - 1:
+                        oevict(h, n, "sv"[n])
+                        store(h, 512 * n, 512 * (n + 1))
+                    else:
+                        oevict(h, n, "s", 0, 256)
+                        oevict(h, n, "v", 256, 512)
+                        store(h, 512 * n, 512 * (n + 1))
+                    if z < NH:
+                        s1h(n + 1, z)
+                if h < NH - 1:
+                    store(h, 0, S)
+                if z == NH - 1:
+                    flush()

@@ -20,6 +20,7 @@ Q = D // 512
 NH = H // P
 NS = S // 512
 WC = 256
+NC = H // WC
 
 FLOPS = 2 * T * D * H + 2 * T * H * S
 BYTES = 2 * T * D + 2 * D * H + 2 * SPK * H + T * S // 2 + T * S // 32 + 4 * H * S
@@ -33,35 +34,44 @@ def tile_lhuc_senone_gradient_s13_kernel(tc, x, w, lhuc, err_words, err_scales, 
         psum = ctx.enter_context(tc.psum_pool(name="psum", bufs=1))
 
         ident = keep.tile([P, P], F32, name="ident")
-        identb = keep.tile([P, P], BF16, name="identb")
-        lrow = keep.tile([P, 512], BF16, name="lrow", align_bytes=64)
-        lcol = keep.tile([P, 4, SPK], BF16, name="lcol", align_bytes=64)
-        lrep = keep.tile([P, 2, G, 2, 2, 64], BF16, name="lrep", align_bytes=64)
-        dummy = keep.tile([P, 1], F32, name="dummy")
-        xraw = [keep.tile([P, 4, D], BF16, name="xraw%d" % g) for g in range(G)]
+        lrow = keep.tile([P, WC], BF16, name="lrow", align_bytes=64)
+        lrep = [keep.tile([P, SPK, 64], F32, name="lrep%d" % c, align_bytes=64) for c in range(2)]
+        lcol = keep.tile([P, SPK, NC], F32, name="lcol")
+        lraw = keep.tile([P, G, 2 * WC], BF16, name="lraw")
+        amp = [keep.tile([P, G, WC], F32, name="amp%d" % c) for c in range(NC)]
         xcod = [keep.tile([P, 4, Q * P], U32, name="xcod%d" % g, align_bytes=64) for g in range(G)]
         xsca = [keep.tile([P, 4, Q * P], U8, name="xsca%d" % g, align_bytes=64) for g in range(G)]
-        wraw = [[keep.tile([P, 4, WC], BF16, name="wraw%d_%d" % (c, q)) for q in range(Q)] for c in range(H // WC)]
-        wcod = [[keep.tile([P, WC], U32, name="wcod%d_%d" % (c, q), align_bytes=64) for q in range(Q)] for c in range(H // WC)]
-        wsca = [[keep.tile([P, WC], U8, name="wsca%d_%d" % (c, q), align_bytes=64) for q in range(Q)] for c in range(H // WC)]
-        lraw = [keep.tile([P, G, 512], BF16, name="lraw%d" % c) for c in range(2)]
-        amp = [keep.tile([P, G, 256], F32, name="amp%d" % c) for c in range(4)]
+        wraw = [[keep.tile([P, 4, WC], BF16, name="wraw%d_%d" % (c, q)) for q in range(Q)] for c in range(NC)]
+        wcod = [[keep.tile([P, WC], U32, name="wcod%d_%d" % (c, q), align_bytes=64) for q in range(Q)] for c in range(NC)]
+        wsca = [[keep.tile([P, WC], U8, name="wsca%d_%d" % (c, q), align_bytes=64) for q in range(Q)] for c in range(NC)]
         hcod = [keep.tile([P, G, P], U32, name="hcod%d" % h, align_bytes=64) for h in range(NH)]
         hsca = [keep.tile([P, G, P], U8, name="hsca%d" % h, align_bytes=64) for h in range(NH)]
         ewor = [keep.tile([P, 2 * S], U8, name="ewor%d" % g, align_bytes=64) for g in range(G)]
         esca = keep.tile([P, G, S], U8, name="esca", align_bytes=64)
 
-        def bank(i):
-            b = psum.tile([P, 512], F32, name="bank%d" % i, tag="bank%d" % i)
+        def bank(i, shape, dtype):
+            b = psum.tile(shape, dtype, name="bank%d" % i, tag="bank%d" % i)
             return b
 
         xbanks = [0, 1, 2, 3]
-        zbanks = [4, 5, 6]
-        obanks = [7, 1, 0, 3, 2]
-        count = {"z": 0, "o": 0}
+        zbanks = [4, 0, 1]
+        obanks = [7, 5, 6, 2, 3]
+        count = {"x": 0, "z": 0, "o": 0}
+
+        def copy_on(eng, dst, src):
+            if eng == "s":
+                nc.scalar.copy(out=dst, in_=src)
+            else:
+                nc.vector.tensor_copy(out=dst, in_=src)
+
+        xraw = {}
 
         def load_x(g, a, b):
-            nc.sync.dma_start(out=xraw[g][:, a:b, :], in_=x[512 * g : 512 * (g + 1), :].rearrange("(m t) k -> m t k", t=4)[:, a:b, :])
+            xt = keep.tile([P, (b - a) * D], BF16, name="xraw%d_%d" % (g, a))
+            rows = x[512 * g : 512 * (g + 1), :].rearrange("(m t) k -> m (t k)", t=4)
+            nc.sync.dma_start(out=xt[:], in_=rows[:, a * D : b * D])
+            for t in range(a, b):
+                xraw[g, t] = xt[:, (t - a) * D : (t - a + 1) * D]
 
         def load_w(c):
             for q in range(Q):
@@ -70,12 +80,12 @@ def tile_lhuc_senone_gradient_s13_kernel(tc, x, w, lhuc, err_words, err_scales, 
                     in_=w[512 * q : 512 * (q + 1), WC * c : WC * (c + 1)].rearrange("(p j) n -> p j n", j=4),
                 )
 
-        def load_lhuc(c, lo, hi):
+        def load_lhuc_spread():
             rows = lhuc.rearrange("(g s) n -> s g n", s=2)
             for s in range(2):
                 nc.sync.dma_start(
-                    out=lraw[c][64 * s : 64 * (s + 1), lo:hi, :],
-                    in_=rows[s, lo:hi, 512 * c : 512 * (c + 1)].partition_broadcast(64),
+                    out=lraw[64 * s : 64 * (s + 1), :, :],
+                    in_=rows[s, :, 2 * WC :].partition_broadcast(64),
                 )
 
         def load_esca():
@@ -89,56 +99,39 @@ def tile_lhuc_senone_gradient_s13_kernel(tc, x, w, lhuc, err_words, err_scales, 
             nc.sync.dma_start(out=ewor[g][:].bitcast(I32), in_=err_words[g].bitcast(I32))
 
         xgrp = {}
-        xord = {}
 
-        def xorder(g, t, eng):
-            xo = work.tile([P, 512], F32, name="xo", tag="xo", bufs=6)
-            dst = xo[:].rearrange("p (q u m) -> p q u m", q=Q, u=2)
-            src = xraw[g][:, t, :].bitcast(F32).rearrange("p (q m u) -> p q u m", q=Q, u=2)
-            if eng == "s":
-                nc.scalar.copy(out=dst, in_=src)
-            else:
-                nc.vector.tensor_copy(out=dst, in_=src)
-            xord[g, t] = xo
-
-        def trans(g, t):
-            b = bank(xbanks[t])
-            words = xraw[g][:, t, :].bitcast(F32)
+        def trans(g, t, eng):
+            b = bank(xbanks[count["x"] % len(xbanks)], [P, 512], F32)
+            count["x"] += 1
+            words = xraw[g, t].bitcast(F32)
             for q in range(Q):
                 for u in range(2):
                     j = 2 * q + u
-                    if (g, t) in xord:
-                        cols = xord[g, t][:, P * j : P * (j + 1)]
-                    else:
-                        cols = words[:, 256 * q + u : 256 * (q + 1) : 2]
-                    nc.tensor.transpose(b[:, P * j : P * (j + 1)], cols, ident[:])
-            xg = work.tile([P, Q, P, 4], BF16, name="xg", tag="xg", align_bytes=64)
-            nc.scalar.copy(
-                out=xg[:].rearrange("p q m t -> p (q m t)").bitcast(F32),
-                in_=b[:].rearrange("p (q u m) -> p q m u", q=Q, u=2),
+                    nc.tensor.transpose(b[:, P * j : P * (j + 1)], words[:, 256 * q + u : 256 * (q + 1) : 2], ident[:])
+            xg = work.tile([P, Q * P * 4], BF16, name="xg", tag="xg", align_bytes=64)
+            copy_on(
+                eng,
+                xg[:].bitcast(F32).rearrange("p (q m u) -> p q m u", q=Q, u=2),
+                b[:].rearrange("p (q u m) -> p q m u", q=Q, u=2),
             )
             xgrp[g, t] = xg
 
         def xquant(g, t):
-            nc.vector.quantize_mx(
-                out=xcod[g][:, t, :].bitcast(FP8X4),
-                scales=xsca[g][:, t, :],
-                in_=xgrp[g, t][:].rearrange("p q m t -> p (q m t)"),
-            )
+            nc.vector.quantize_mx(out=xcod[g][:, t, :].bitcast(FP8X4), scales=xsca[g][:, t, :], in_=xgrp[g, t][:])
 
         wgrp = {}
 
-        def winter(h, q, eng, n=1):
+        def winter(h, q, eng, n):
             c, off = divmod(P * h, WC)
             wg = work.tile([P, P * n, 4], BF16, name="wg", tag="wg", align_bytes=64)
-            src = wraw[c][q][:, :, off : off + P * n].rearrange("p j n -> p n j")
-            if eng == "s":
-                nc.scalar.copy(out=wg[:], in_=src)
-            else:
-                nc.vector.tensor_copy(out=wg[:], in_=src)
+            copy_on(
+                eng,
+                wg[:].rearrange("p (c i) j -> p c j i", i=4),
+                wraw[c][q][:, :, off : off + P * n].rearrange("p j (c i) -> p c j i", i=4),
+            )
             wgrp[h, q] = wg
 
-        def wquant(h, q, n=1):
+        def wquant(h, q, n):
             c, off = divmod(P * h, WC)
             nc.vector.quantize_mx(
                 out=wcod[c][q][:, off : off + P * n].bitcast(FP8X4),
@@ -146,36 +139,38 @@ def tile_lhuc_senone_gradient_s13_kernel(tc, x, w, lhuc, err_words, err_scales, 
                 in_=wgrp[h, q][:].rearrange("p n j -> p (n j)"),
             )
 
+        abank = {}
+
         def lhuc_turn():
-            b = psum.tile([P, 4, P], BF16, name="bank5l", tag="bank5")
-            for h in range(4):
-                nc.tensor.transpose(b[:, h, :], lrow[:, P * h : P * (h + 1)], identb[:])
-            nc.vector.tensor_copy(out=lcol[:], in_=b[:, :, 0:SPK])
+            b = bank(7, [P, P], F32)
+            nc.tensor.transpose(b[:], lrow[:].bitcast(F32), ident[:])
+            nc.vector.tensor_copy(out=lcol[:].rearrange("p s c -> p (s c)"), in_=b[:, 0 : SPK * NC])
+            for c in range(2):
+                nc.vector.tensor_copy(out=lrep[c][:], in_=lcol[:, :, c : c + 1].to_broadcast([P, SPK, 64]))
 
-        def lhuc_repeat(a, g, eng):
-            src = lcol[:, 2 * a : 2 * (a + 1), 2 * g : 2 * (g + 1)].unsqueeze(3).to_broadcast([P, 2, 2, 64])
-            if eng == "s":
-                nc.scalar.copy(out=lrep[:, a, g, :, :, :], in_=src)
-            else:
-                nc.vector.tensor_copy(out=lrep[:, a, g, :, :, :], in_=src)
-
-        def lhuc_spread(a, lo, hi, i):
-            b = psum.tile([P, G, 256], BF16, name="bank%dl" % i, tag="bank%d" % i)
-            for g in range(lo, hi):
-                for h in range(2):
-                    nc.tensor.transpose(
-                        b[:, g, P * h : P * (h + 1)], lrep[:, a, g, h, :, :].rearrange("p s r -> p (s r)"), identb[:]
-                    )
-            nc.scalar.activation(out=amp[a][:, lo:hi, :], in_=b[:, lo:hi, :], func=ACT.Sigmoid)
+        def lhuc_spread(c):
+            b = bank(5 + c, [P, G, P], F32)
+            for g in range(G):
+                nc.tensor.transpose(b[:, g, :], lrep[c][:, 2 * g : 2 * g + 2, :].rearrange("p s r -> p (s r)"), ident[:])
+            abank[c] = b
 
         def sigm(c, lo, hi):
-            nc.scalar.activation(out=amp[c][:, lo:hi, :], in_=lraw[c // 2][:, lo:hi, 256 * (c % 2) : 256 * (c % 2 + 1)], func=ACT.Sigmoid)
+            if c < 2:
+                src = abank[c][:, lo:hi, :].bitcast(BF16)
+            else:
+                src = lraw[:, lo:hi, WC * (c - 2) : WC * (c - 1)]
+            nc.scalar.activation(out=amp[c][:, lo:hi, :], in_=src, func=ACT.Sigmoid)
 
-        zb = {}
-        hgrp = {}
+        pend = []
+
+        def hquant():
+            g, h, hg = pend.pop(0)
+            nc.vector.quantize_mx(
+                out=hcod[h][:, g, :].bitcast(FP8X4), scales=hsca[h][:, g, :], in_=hg[:].rearrange("p n t -> p (n t)")
+            )
 
         def s1(g, h):
-            z = bank(zbanks[count["z"] % len(zbanks)])
+            z = bank(zbanks[count["z"] % len(zbanks)], [P, 512], F32)
             count["z"] += 1
             c, off = divmod(P * h, WC)
             for t in range(4):
@@ -189,194 +184,129 @@ def tile_lhuc_senone_gradient_s13_kernel(tc, x, w, lhuc, err_words, err_scales, 
                         start=(q == 0),
                         stop=(q == Q - 1),
                     )
-            zb[g, h] = z
-
-        def hevict(g, h):
-            c, off = divmod(P * h, 256)
             hg = work.tile([P, P, 4], BF16, name="hg", tag="hg", align_bytes=64)
             nc.vector.scalar_tensor_tensor(
                 out=hg[:],
-                in0=zb[g, h][:].rearrange("p (t n) -> p n t", t=4),
+                in0=z[:].rearrange("p (t n) -> p n t", t=4),
                 scalar=0.0,
                 in1=amp[c][:, g, off : off + P].unsqueeze(2).to_broadcast([P, P, 4]),
                 op0=ALU.max,
                 op1=ALU.mult,
             )
-            hgrp[g, h] = hg
-
-        def hquant(g, h):
-            nc.vector.quantize_mx(
-                out=hcod[h][:, g, :].bitcast(FP8X4),
-                scales=hsca[h][:, g, :],
-                in_=hgrp[g, h][:].rearrange("p n t -> p (n t)"),
-            )
-
-        pend = []
-
-        def s1h(g, h):
-            s1(g, h)
-            hevict(g, h)
             if pend:
-                hquant(*pend.pop())
-            pend.append((g, h))
-
-        def flush():
-            if pend:
-                hquant(*pend.pop())
+                hquant()
+            pend.append((g, h, hg))
 
         ob = {}
         og = {}
 
-        def s2(h, n, groups):
+        def s2(h, lo, hi, groups):
             if groups[0] == 0:
-                ob[h, n] = bank(obanks[count["o"] % len(obanks)])
+                ob[h, lo] = bank(obanks[count["o"] % len(obanks)], [P, hi - lo], F32)
                 count["o"] += 1
             for g in groups:
                 nc.tensor.matmul_mx(
-                    out=ob[h, n][:],
+                    out=ob[h, lo][:],
                     lhsT=hcod[h][:, g, :].bitcast(FP8X4),
                     lhsT_scale=hsca[h][:, g, :],
-                    rhs=ewor[g][:, 1024 * n : 1024 * (n + 1)].bitcast(FP4X4),
-                    rhs_scale=esca[:, g, 512 * n : 512 * (n + 1)],
+                    rhs=ewor[g][:, 2 * lo : 2 * hi].bitcast(FP4X4),
+                    rhs_scale=esca[:, g, lo:hi],
                     start=(g == 0),
                     stop=(g == G - 1),
                 )
 
-        def oevict(h, n, eng, lo=0, hi=512):
+        def oevict(h, lo, hi, eng):
             if h not in og:
                 og[h] = work.tile([P, S], F32, name="og", tag="og", bufs=3)
-            dst = og[h][:, 512 * n + lo : 512 * n + hi]
-            src = ob[h, n][:, lo:hi]
+            dst = og[h][:, lo:hi]
             if eng == "s":
-                nc.scalar.activation(out=dst, in_=src, func=ACT.Copy, scale=2.0)
+                nc.scalar.activation(out=dst, in_=ob[h, lo][:], func=ACT.Copy, scale=2.0)
             else:
-                nc.vector.tensor_scalar(out=dst, in0=src, scalar1=2.0, scalar2=None, op0=ALU.mult)
+                nc.vector.tensor_scalar(out=dst, in0=ob[h, lo][:], scalar1=2.0, scalar2=None, op0=ALU.mult)
 
         def store(h, lo, hi):
             nc.sync.dma_start(out=out[P * h : P * (h + 1), lo:hi], in_=og[h][:, lo:hi])
 
         with tc.manual_schedule():
-            nc.vector.memset(dummy[:], 0.0)
-            nc.vector.memset(lrow[:], 0.0)
-            nc.scalar.dma_start(out=lrow[0:SPK, :], in_=lhuc[:, 0:512])
-            nc.scalar.activation(out=dummy[:], in_=dummy[:], func=ACT.Sigmoid)
+            nc.scalar.dma_start(out=lrow[0:32, :], in_=lhuc.rearrange("s (c n) -> (s c) n", n=WC))
+            nc.vector.memset(lrow[32:64, :], 0.0)
+            nc.vector.memset(lrow[64:128, :], 0.0)
             make_identity(nc, ident[:])
-            make_identity(nc, identb[:])
             nc.vector.memset(esca[:].rearrange("p g n -> p (g n)").bitcast(I32), 0)
-            load_x(0, 0, 1)
-            load_x(0, 1, 2)
-            load_x(0, 2, 3)
-            load_x(0, 3, 4)
             load_w(0)
-            load_x(1, 0, 2)
-            load_x(1, 2, 4)
-            load_x(2, 0, 4)
-            load_x(3, 0, 4)
-            load_w(1)
+            for t in range(4):
+                load_x(0, t, t + 1)
+            for g in range(1, G):
+                load_x(g, 0, 2)
+                load_x(g, 2, 4)
             load_esca()
-            for g in range(G):
-                load_ewor(g)
+            load_ewor(0)
+            load_ewor(1)
+            load_w(1)
+            load_ewor(2)
+            load_ewor(3)
             load_w(2)
             load_w(3)
-            load_lhuc(1, 0, 4)
+            load_lhuc_spread()
 
-            trans(0, 0)
-            trans(0, 1)
             lhuc_turn()
-            lhuc_repeat(0, 0, "v")
-            trans(0, 2)
-            trans(0, 3)
-            xquant(0, 0)
-            xquant(0, 1)
-            winter(0, 0, "v")
-            winter(0, 1, "v")
-            xquant(0, 2)
-            wquant(0, 0)
-            wquant(0, 1)
-            xquant(0, 3)
-            lhuc_spread(0, 0, 1, 7)
-            winter(1, 0, "s")
-            winter(1, 1, "v")
-            lhuc_repeat(0, 1, "v")
-            wquant(1, 1)
-            wquant(1, 0)
-            lhuc_repeat(0, 2, "v")
-            lhuc_repeat(0, 3, "v")
-            s1h(0, 0)
-            trans(1, 0)
-            xquant(1, 0)
-            trans(1, 1)
-            xquant(1, 1)
-            xorder(2, 0, "v")
-            trans(1, 2)
-            xquant(1, 2)
-            xorder(2, 1, "v")
-            trans(1, 3)
-            xquant(1, 3)
-            xorder(2, 2, "v")
-            xorder(2, 3, "v")
-            lhuc_spread(0, 1, 4, 6)
-            s1h(0, 1)
-            for t in range(4):
-                trans(2, t)
-                xquant(2, t)
-                if t % 2:
-                    xorder(3, t, "v")
-            xorder(3, 0, "s")
-            s1h(1, 0)
-            s1h(1, 1)
-            for t in (1, 0, 3, 2):
-                trans(3, t)
-                xquant(3, t)
-            s1h(2, 0)
-            winter(2, 0, "s")
-            s1h(2, 1)
-            for g in (0, 1):
-                for n in range(NS):
-                    s2(0, n, [g])
-            winter(2, 1, "s")
+            lhuc_spread(0)
+            lhuc_spread(1)
+            for q in range(Q):
+                winter(0, q, "v", 2)
+            for q in range(Q):
+                wquant(0, q, 2)
+            sigm(0, 0, G)
+            prev = None
             for g in range(G):
-                lhuc_repeat(1, g, "s")
-            wquant(2, 0)
-            wquant(2, 1)
-            s1h(3, 0)
-            s1h(3, 1)
-            flush()
-            lhuc_spread(1, 0, 4, 3)
-            winter(3, 0, "s")
-            winter(3, 1, "v")
-            wquant(3, 0)
-            wquant(3, 1)
-            for h in range(NH):
-                z = h + 2
-                if z < NH:
-                    s1h(0, z)
-                if z == 3:
-                    winter(4, 0, "s", 2)
-                    winter(4, 1, "s", 2)
-                    sigm(2, 0, 4)
-                    wquant(4, 0, 2)
-                    wquant(4, 1, 2)
-                if z == 5:
-                    sigm(3, 0, 4)
-                    winter(6, 0, "s", 2)
-                    winter(6, 1, "s", 2)
-                    wquant(6, 0, 2)
-                    wquant(6, 1, 2)
+                for t in range(4):
+                    trans(g, t, "v" if t == 2 else "s")
+                    if prev:
+                        xquant(*prev)
+                    prev = (g, t)
+            s1(0, 0)
+            xquant(*prev)
+            sigm(1, 0, G)
+            for g in range(1, G):
+                s1(g, 0)
+            for q in range(Q):
+                winter(2, q, "s", 1)
+            for g in range(G):
+                if g == G - 2:
+                    for q in range(Q):
+                        wquant(2, q, 1)
                 for n in range(NS):
-                    s2(h, n, [2, 3] if h == 0 else [0, 1, 2, 3])
-                    if h < NH - 1:
-                        oevict(h, n, "s")
-                    elif n < NS - 1:
-                        oevict(h, n, "sv"[n])
-                        store(h, 512 * n, 512 * (n + 1))
-                    else:
-                        oevict(h, n, "s", 0, 256)
-                        oevict(h, n, "v", 256, 512)
-                        store(h, 512 * n, 512 * (n + 1))
-                    if z < NH:
-                        s1h(n + 1, z)
+                    s2(0, 512 * n, 512 * (n + 1), [g])
+                s1(g, 1)
+            for n in range(NS):
+                oevict(0, 512 * n, 512 * (n + 1), "s")
+            store(0, 0, S)
+            for h in range(1, NH):
+                z = h + 1
+                nxt = h + 2
+                if z < NH:
+                    s1(0, z)
+                    s1(1, z)
+                else:
+                    hquant()
+                if nxt < NH:
+                    for q in range(Q):
+                        winter(nxt, q, "s", 1)
                 if h < NH - 1:
-                    store(h, 0, S)
-                if z == NH - 1:
-                    flush()
+                    for n in range(NS):
+                        s2(h, 512 * n, 512 * (n + 1), range(G))
+                        oevict(h, 512 * n, 512 * (n + 1), "s")
+                        store(h, 512 * n, 512 * (n + 1))
+                        if n < 2:
+                            s1(n + 2, z)
+                        if n == 0 and nxt < NH:
+                            for q in range(Q):
+                                wquant(nxt, q, 1)
+                        if n == 1 and nxt % 2 == 0 and 4 <= nxt < NH:
+                            sigm(nxt // 2, 0, G)
+                else:
+                    cuts = [0, 512, 768, 1024, 1280, 1408, S]
+                    for i in range(len(cuts) - 1):
+                        s2(h, cuts[i], cuts[i + 1], range(G))
+                        oevict(h, cuts[i], cuts[i + 1], "sv"[i % 2])
+                        store(h, cuts[i], cuts[i + 1])

@@ -37,15 +37,15 @@ def tile_lhuc_senone_gradient_s13_kernel(tc, x, w, lhuc, err_words, err_scales, 
         lrow = keep.tile([P, WC], BF16, name="lrow", align_bytes=64)
         lrep = [keep.tile([P, SPK, 64], F32, name="lrep%d" % c, align_bytes=64) for c in range(2)]
         lcol = keep.tile([P, SPK, NC], F32, name="lcol")
-        lraw = keep.tile([P, G, 2 * WC], BF16, name="lraw")
+        lraw = [keep.tile([P, G, WC], BF16, name="lraw%d" % c) for c in range(2)]
         amp = [keep.tile([P, G, WC], F32, name="amp%d" % c) for c in range(NC)]
         xcod = [keep.tile([P, 4, Q * P], U32, name="xcod%d" % g, align_bytes=64) for g in range(G)]
         xsca = [keep.tile([P, 4, Q * P], U8, name="xsca%d" % g, align_bytes=64) for g in range(G)]
         wraw = [[keep.tile([P, 4, WC], BF16, name="wraw%d_%d" % (c, q)) for q in range(Q)] for c in range(NC)]
         wcod = [[keep.tile([P, WC], U32, name="wcod%d_%d" % (c, q), align_bytes=64) for q in range(Q)] for c in range(NC)]
         wsca = [[keep.tile([P, WC], U8, name="wsca%d_%d" % (c, q), align_bytes=64) for q in range(Q)] for c in range(NC)]
-        hcod = [keep.tile([P, G, P], U32, name="hcod%d" % h, align_bytes=64) for h in range(NH)]
-        hsca = [keep.tile([P, G, P], U8, name="hsca%d" % h, align_bytes=64) for h in range(NH)]
+        hcod = [keep.tile([P, G, WC], U32, name="hcod%d" % c, align_bytes=64) for c in range(NC)]
+        hsca = [keep.tile([P, G, WC], U8, name="hsca%d" % c, align_bytes=64) for c in range(NC)]
         ewor = [keep.tile([P, 2 * S], U8, name="ewor%d" % g, align_bytes=64) for g in range(G)]
         esca = keep.tile([P, G, S], U8, name="esca", align_bytes=64)
 
@@ -54,8 +54,8 @@ def tile_lhuc_senone_gradient_s13_kernel(tc, x, w, lhuc, err_words, err_scales, 
             return b
 
         xbanks = [0, 1, 2, 3]
-        zbanks = [4, 0, 1]
-        obanks = [7, 5, 6, 2, 3]
+        zbanks = [4, 7]
+        obanks = [5, 2, 3, 6]
         count = {"x": 0, "z": 0, "o": 0}
 
         def copy_on(eng, dst, src):
@@ -80,12 +80,12 @@ def tile_lhuc_senone_gradient_s13_kernel(tc, x, w, lhuc, err_words, err_scales, 
                     in_=w[512 * q : 512 * (q + 1), WC * c : WC * (c + 1)].rearrange("(p j) n -> p j n", j=4),
                 )
 
-        def load_lhuc_spread():
+        def load_lhuc_spread(c):
             rows = lhuc.rearrange("(g s) n -> s g n", s=2)
             for s in range(2):
                 nc.sync.dma_start(
-                    out=lraw[64 * s : 64 * (s + 1), :, :],
-                    in_=rows[s, :, 2 * WC :].partition_broadcast(64),
+                    out=lraw[c - 2][64 * s : 64 * (s + 1), :, :],
+                    in_=rows[s, :, WC * c : WC * (c + 1)].partition_broadcast(64),
                 )
 
         def load_esca():
@@ -158,44 +158,53 @@ def tile_lhuc_senone_gradient_s13_kernel(tc, x, w, lhuc, err_words, err_scales, 
             if c < 2:
                 src = abank[c][:, lo:hi, :].bitcast(BF16)
             else:
-                src = lraw[:, lo:hi, WC * (c - 2) : WC * (c - 1)]
+                src = lraw[c - 2][:, lo:hi, :]
             nc.scalar.activation(out=amp[c][:, lo:hi, :], in_=src, func=ACT.Sigmoid)
 
-        pend = []
+        halves = {}
+        zb = {}
+        hgrp = {}
 
-        def hquant():
-            g, h, hg = pend.pop(0)
-            nc.vector.quantize_mx(
-                out=hcod[h][:, g, :].bitcast(FP8X4), scales=hsca[h][:, g, :], in_=hg[:].rearrange("p n t -> p (n t)")
-            )
-
-        def s1(g, h):
-            z = bank(zbanks[count["z"] % len(zbanks)], [P, 512], F32)
+        def s1(g, c, u):
+            if u == 0:
+                halves[g, c] = work.tile([P, 2, WC, 2], BF16, name="half", tag="half", bufs=3, align_bytes=64)
+            z = bank(zbanks[count["z"] % len(zbanks)], [P, 2, WC], F32)
             count["z"] += 1
-            c, off = divmod(P * h, WC)
-            for t in range(4):
+            for e in range(2):
+                t = 2 * u + e
                 for q in range(Q):
                     nc.tensor.matmul_mx(
-                        out=z[:, P * t : P * (t + 1)],
+                        out=z[:, e, :],
                         lhsT=xcod[g][:, t, P * q : P * (q + 1)].bitcast(FP8X4),
                         lhsT_scale=xsca[g][:, t, P * q : P * (q + 1)],
-                        rhs=wcod[c][q][:, off : off + P].bitcast(FP8X4),
-                        rhs_scale=wsca[c][q][:, off : off + P],
+                        rhs=wcod[c][q][:].bitcast(FP8X4),
+                        rhs_scale=wsca[c][q][:],
                         start=(q == 0),
                         stop=(q == Q - 1),
                     )
-            hg = work.tile([P, P, 4], BF16, name="hg", tag="hg", align_bytes=64)
+            zb[g, c, u] = z
+
+        def hevict(g, c, u):
             nc.vector.scalar_tensor_tensor(
-                out=hg[:],
-                in0=z[:].rearrange("p (t n) -> p n t", t=4),
+                out=halves[g, c][:, u, :, :],
+                in0=zb[g, c, u][:].rearrange("p e n -> p n e"),
                 scalar=0.0,
-                in1=amp[c][:, g, off : off + P].unsqueeze(2).to_broadcast([P, P, 4]),
+                in1=amp[c][:, g, :].unsqueeze(2).to_broadcast([P, WC, 2]),
                 op0=ALU.max,
                 op1=ALU.mult,
             )
-            if pend:
-                hquant()
-            pend.append((g, h, hg))
+
+        def hjoin(g, c, eng):
+            hg = work.tile([P, WC * 4], BF16, name="hg", tag="hg", bufs=3, align_bytes=64)
+            copy_on(
+                eng,
+                hg[:].bitcast(F32).rearrange("p (n u) -> p n u", u=2),
+                halves[g, c][:].rearrange("p u n e -> p (u n e)").bitcast(F32).rearrange("p (u n) -> p n u", u=2),
+            )
+            hgrp[g, c] = hg
+
+        def hquant(g, c):
+            nc.vector.quantize_mx(out=hcod[c][:, g, :].bitcast(FP8X4), scales=hsca[c][:, g, :], in_=hgrp[g, c][:])
 
         ob = {}
         og = {}
@@ -207,8 +216,8 @@ def tile_lhuc_senone_gradient_s13_kernel(tc, x, w, lhuc, err_words, err_scales, 
             for g in groups:
                 nc.tensor.matmul_mx(
                     out=ob[h, lo][:],
-                    lhsT=hcod[h][:, g, :].bitcast(FP8X4),
-                    lhsT_scale=hsca[h][:, g, :],
+                    lhsT=hcod[h // 2][:, g, P * (h % 2) : P * (h % 2 + 1)].bitcast(FP8X4),
+                    lhsT_scale=hsca[h // 2][:, g, P * (h % 2) : P * (h % 2 + 1)],
                     rhs=ewor[g][:, 2 * lo : 2 * hi].bitcast(FP4X4),
                     rhs_scale=esca[:, g, lo:hi],
                     start=(g == 0),
@@ -233,80 +242,124 @@ def tile_lhuc_senone_gradient_s13_kernel(tc, x, w, lhuc, err_words, err_scales, 
             nc.vector.memset(lrow[64:128, :], 0.0)
             make_identity(nc, ident[:])
             nc.vector.memset(esca[:].rearrange("p g n -> p (g n)").bitcast(I32), 0)
-            load_w(0)
             for t in range(4):
                 load_x(0, t, t + 1)
+            load_w(0)
             for g in range(1, G):
                 load_x(g, 0, 2)
                 load_x(g, 2, 4)
-            load_esca()
-            load_ewor(0)
-            load_ewor(1)
             load_w(1)
-            load_ewor(2)
-            load_ewor(3)
-            load_w(2)
-            load_w(3)
-            load_lhuc_spread()
+            load_esca()
+            for g in range(G):
+                load_ewor(g)
+            for c in (2, 3):
+                load_w(c)
+                load_lhuc_spread(c)
 
             lhuc_turn()
-            lhuc_spread(0)
-            lhuc_spread(1)
-            for q in range(Q):
-                winter(0, q, "v", 2)
-            for q in range(Q):
-                wquant(0, q, 2)
-            sigm(0, 0, G)
-            prev = None
-            for g in range(G):
-                for t in range(4):
-                    trans(g, t, "v" if t == 2 else "s")
-                    if prev:
-                        xquant(*prev)
-                    prev = (g, t)
-            s1(0, 0)
-            xquant(*prev)
-            sigm(1, 0, G)
-            for g in range(1, G):
-                s1(g, 0)
-            for q in range(Q):
-                winter(2, q, "s", 1)
-            for g in range(G):
-                if g == G - 2:
-                    for q in range(Q):
-                        wquant(2, q, 1)
+            for k in range(2 * G):
+                g, u = divmod(k, 2)
+                trans(g, 2 * u, "s" if k else "v")
+                if k == 0:
+                    lhuc_spread(0)
+                    sigm(0, 0, 1)
+                trans(g, 2 * u + 1, "s")
+                if k == 1:
+                    lhuc_spread(1)
+                    sigm(0, 1, G)
+                if k == 2:
+                    s1(0, 0, 0)
+                if k >= 2:
+                    s1((k - 1) // 2, 0, (k - 1) % 2)
+                if k >= 3 and u == 1:
+                    hjoin(g - 1, 0, "s")
+                if k >= 4 and u == 0:
+                    hquant(g - 2, 0)
+                xquant(g, 2 * u)
+                if k == 0:
+                    winter(0, 0, "v", 2)
+                    winter(0, 1, "v", 2)
+                    wquant(0, 0, 2)
+                xquant(g, 2 * u + 1)
+                if k == 0:
+                    wquant(0, 1, 2)
+                if k == 2:
+                    hevict(0, 0, 0)
+                if k >= 2:
+                    hevict((k - 1) // 2, 0, (k - 1) % 2)
+                if k in (4, 6):
+                    sigm(1, k - 4, k - 2)
+                if k in (5, 6):
+                    winter(2, k - 5, "v", 2)
+                if k in (6, 7):
+                    wquant(2, k - 6, 2)
+            zbanks.extend([0, 1])
+
+            def stage(k, c):
+                g, u = divmod(k, 2)
+                s1(g, c, u)
+                hevict(g, c, u)
+                if u == 1:
+                    hjoin(g, c, "s")
+                    if g > 0 and c > 0:
+                        hquant(g - 1, c)
+
+            def finish(h, n):
+                oevict(h, 512 * n, 512 * (n + 1), "s")
+                store(h, 512 * n, 512 * (n + 1))
+
+            for g in range(2):
                 for n in range(NS):
                     s2(0, 512 * n, 512 * (n + 1), [g])
-                s1(g, 1)
+            hquant(G - 2, 0)
+            stage(2 * G - 1, 0)
+            stage(0, 1)
+            hquant(G - 1, 0)
             for n in range(NS):
-                oevict(0, 512 * n, 512 * (n + 1), "s")
-            store(0, 0, S)
-            for h in range(1, NH):
-                z = h + 1
-                nxt = h + 2
-                if z < NH:
-                    s1(0, z)
-                    s1(1, z)
-                else:
-                    hquant()
-                if nxt < NH:
-                    for q in range(Q):
-                        winter(nxt, q, "s", 1)
-                if h < NH - 1:
-                    for n in range(NS):
-                        s2(h, 512 * n, 512 * (n + 1), range(G))
-                        oevict(h, 512 * n, 512 * (n + 1), "s")
-                        store(h, 512 * n, 512 * (n + 1))
-                        if n < 2:
-                            s1(n + 2, z)
-                        if n == 0 and nxt < NH:
-                            for q in range(Q):
-                                wquant(nxt, q, 1)
-                        if n == 1 and nxt % 2 == 0 and 4 <= nxt < NH:
-                            sigm(nxt // 2, 0, G)
-                else:
-                    cuts = [0, 512, 768, 1024, 1280, 1408, S]
-                    for i in range(len(cuts) - 1):
-                        s2(h, cuts[i], cuts[i + 1], range(G))
-                        oevict(h, cuts[i], cuts[i + 1], "sv"[i % 2])
-                        store(h, cuts[i], cuts[i + 1])
+                s2(0, 512 * n, 512 * (n + 1), [2])
+            stage(1, 1)
+            stage(2, 1)
+            for q in range(Q):
+                winter(4, q, "v", 2)
+            for n in range(NS):
+                s2(0, 512 * n, 512 * (n + 1), [3])
+                finish(0, n)
+            k = 3
+            for n in range(NS):
+                for j in range(2 if n < 2 else 1):
+                    stage(k, 1)
+                    k += 1
+                s2(1, 512 * n, 512 * (n + 1), range(G))
+                finish(1, n)
+                if n < Q:
+                    wquant(4, n, 2)
+                if n >= 1:
+                    sigm(2, 2 * n - 2, 2 * n)
+            hquant(G - 1, 1)
+            share = [1, 2, 2, 2, 1, 0]
+            for c in range(1, NC):
+                k = 0
+                for i in range(2 * NS):
+                    h, n = 2 * c + i // NS, i % NS
+                    if c + 1 < NC:
+                        for j in range(share[i]):
+                            stage(k, c + 1)
+                            k += 1
+                    if i == 5 and c + 1 < NC:
+                        hquant(G - 1, c + 1)
+                    if h == NH - 1:
+                        break
+                    s2(h, 512 * n, 512 * (n + 1), range(G))
+                    finish(h, n)
+                    if c + 2 < NC:
+                        if i in (1, 2):
+                            winter(2 * c + 4, i - 1, "v", 2)
+                        if i in (3, 4):
+                            wquant(2 * c + 4, i - 3, 2)
+                        if i == 4:
+                            sigm(c + 2, 0, G)
+            cuts = [0, 512, 768, 1024, 1280, 1408, S]
+            for i in range(len(cuts) - 1):
+                s2(NH - 1, cuts[i], cuts[i + 1], range(G))
+                oevict(NH - 1, cuts[i], cuts[i + 1], "sv"[i % 2])
+                store(NH - 1, cuts[i], cuts[i + 1])

@@ -53,9 +53,9 @@ def tile_lhuc_senone_gradient_s13_kernel(tc, x, w, lhuc, err_words, err_scales, 
             b = psum.tile(shape, dtype, name="bank%d" % i, tag="bank%d" % i)
             return b
 
-        xbanks = [0, 1, 2, 3]
+        xbanks = [0, 1, 2]
         zbanks = [4, 7]
-        obanks = [5, 2, 3, 6]
+        obanks = [3, 5, 6]
         count = {"x": 0, "z": 0, "o": 0}
 
         def copy_on(eng, dst, src):
@@ -99,25 +99,48 @@ def tile_lhuc_senone_gradient_s13_kernel(tc, x, w, lhuc, err_words, err_scales, 
             nc.sync.dma_start(out=ewor[g][:].bitcast(I32), in_=err_words[g].bitcast(I32))
 
         xgrp = {}
+        xord = {}
 
-        def trans(g, t, eng):
+        def xsort(g, t, eng):
+            xo = work.tile([P, 512], F32, name="xo", tag="xo", bufs=4)
+            copy_on(
+                eng,
+                xo[:].rearrange("p (q u m) -> p q u m", q=Q, u=2),
+                xraw[g, t].bitcast(F32).rearrange("p (q m u) -> p q u m", q=Q, u=2),
+            )
+            xord[g, t] = xo
+
+        def trans(g, t):
             b = bank(xbanks[count["x"] % len(xbanks)], [P, 512], F32)
             count["x"] += 1
             words = xraw[g, t].bitcast(F32)
             for q in range(Q):
                 for u in range(2):
                     j = 2 * q + u
-                    nc.tensor.transpose(b[:, P * j : P * (j + 1)], words[:, 256 * q + u : 256 * (q + 1) : 2], ident[:])
-            xg = work.tile([P, Q * P * 4], BF16, name="xg", tag="xg", align_bytes=64)
+                    if (g, t) in xord:
+                        cols = xord[g, t][:, P * j : P * (j + 1)]
+                    else:
+                        cols = words[:, 256 * q + u : 256 * (q + 1) : 2]
+                    nc.tensor.transpose(b[:, P * j : P * (j + 1)], cols, ident[:])
+            xbank[g, t] = b
+
+        xbank = {}
+
+        def xevict(g, t, eng):
+            if t % 2 == 0:
+                xgrp[g, t // 2] = work.tile([P, 2 * D], BF16, name="xg", tag="xg", bufs=3, align_bytes=64)
             copy_on(
                 eng,
-                xg[:].bitcast(F32).rearrange("p (q m u) -> p q m u", q=Q, u=2),
-                b[:].rearrange("p (q u m) -> p q m u", q=Q, u=2),
+                xgrp[g, t // 2][:, D * (t % 2) : D * (t % 2 + 1)].bitcast(F32).rearrange("p (q m u) -> p q m u", q=Q, u=2),
+                xbank[g, t][:].rearrange("p (q u m) -> p q m u", q=Q, u=2),
             )
-            xgrp[g, t] = xg
 
         def xquant(g, t):
-            nc.vector.quantize_mx(out=xcod[g][:, t, :].bitcast(FP8X4), scales=xsca[g][:, t, :], in_=xgrp[g, t][:])
+            nc.vector.quantize_mx(
+                out=xcod[g][:, t, :].bitcast(FP8X4),
+                scales=xsca[g][:, t, :],
+                in_=xgrp[g, t // 2][:, D * (t % 2) : D * (t % 2 + 1)],
+            )
 
         wgrp = {}
 
@@ -145,8 +168,9 @@ def tile_lhuc_senone_gradient_s13_kernel(tc, x, w, lhuc, err_words, err_scales, 
             b = bank(7, [P, P], F32)
             nc.tensor.transpose(b[:], lrow[:].bitcast(F32), ident[:])
             nc.vector.tensor_copy(out=lcol[:].rearrange("p s c -> p (s c)"), in_=b[:, 0 : SPK * NC])
-            for c in range(2):
-                nc.vector.tensor_copy(out=lrep[c][:], in_=lcol[:, :, c : c + 1].to_broadcast([P, SPK, 64]))
+
+        def lhuc_repeat(c):
+            nc.vector.tensor_copy(out=lrep[c][:], in_=lcol[:, :, c : c + 1].to_broadcast([P, SPK, 64]))
 
         def lhuc_spread(c):
             b = bank(5 + c, [P, G, P], F32)
@@ -245,55 +269,21 @@ def tile_lhuc_senone_gradient_s13_kernel(tc, x, w, lhuc, err_words, err_scales, 
             for t in range(4):
                 load_x(0, t, t + 1)
             load_w(0)
-            for g in range(1, G):
-                load_x(g, 0, 2)
-                load_x(g, 2, 4)
-            load_w(1)
+            load_x(1, 0, 2)
+            load_x(1, 2, 4)
+            load_x(2, 0, 2)
+            load_x(2, 2, 4)
             load_esca()
-            for g in range(G):
+            load_ewor(0)
+            load_x(3, 0, 2)
+            load_x(3, 2, 4)
+            load_ewor(1)
+            load_w(1)
+            for g in range(2, G):
                 load_ewor(g)
             for c in (2, 3):
                 load_w(c)
                 load_lhuc_spread(c)
-
-            lhuc_turn()
-            for k in range(2 * G):
-                g, u = divmod(k, 2)
-                trans(g, 2 * u, "s" if k else "v")
-                if k == 0:
-                    lhuc_spread(0)
-                    sigm(0, 0, 1)
-                trans(g, 2 * u + 1, "s")
-                if k == 1:
-                    lhuc_spread(1)
-                    sigm(0, 1, G)
-                if k == 2:
-                    s1(0, 0, 0)
-                if k >= 2:
-                    s1((k - 1) // 2, 0, (k - 1) % 2)
-                if k >= 3 and u == 1:
-                    hjoin(g - 1, 0, "s")
-                if k >= 4 and u == 0:
-                    hquant(g - 2, 0)
-                xquant(g, 2 * u)
-                if k == 0:
-                    winter(0, 0, "v", 2)
-                    winter(0, 1, "v", 2)
-                    wquant(0, 0, 2)
-                xquant(g, 2 * u + 1)
-                if k == 0:
-                    wquant(0, 1, 2)
-                if k == 2:
-                    hevict(0, 0, 0)
-                if k >= 2:
-                    hevict((k - 1) // 2, 0, (k - 1) % 2)
-                if k in (4, 6):
-                    sigm(1, k - 4, k - 2)
-                if k in (5, 6):
-                    winter(2, k - 5, "v", 2)
-                if k in (6, 7):
-                    wquant(2, k - 6, 2)
-            zbanks.extend([0, 1])
 
             def stage(k, c):
                 g, u = divmod(k, 2)
@@ -308,34 +298,118 @@ def tile_lhuc_senone_gradient_s13_kernel(tc, x, w, lhuc, err_words, err_scales, 
                 oevict(h, 512 * n, 512 * (n + 1), "s")
                 store(h, 512 * n, 512 * (n + 1))
 
-            for g in range(2):
-                for n in range(NS):
-                    s2(0, 512 * n, 512 * (n + 1), [g])
-            hquant(G - 2, 0)
-            stage(2 * G - 1, 0)
-            stage(0, 1)
-            hquant(G - 1, 0)
-            for n in range(NS):
-                s2(0, 512 * n, 512 * (n + 1), [2])
-            stage(1, 1)
-            stage(2, 1)
+            def s2row(h, g, banks):
+                for n in banks:
+                    s2(h, 512 * n, 512 * (n + 1), [g])
+
+            lhuc_turn()
+            lhuc_repeat(0)
+            trans(0, 0)
+            xsort(0, 1, "v")
+            lhuc_spread(0)
+            sigm(0, 0, 1)
+            xevict(0, 0, "s")
+            xsort(0, 2, "v")
+            lhuc_repeat(1)
+            trans(0, 1)
+            xsort(0, 3, "v")
+            xevict(0, 1, "s")
+            trans(0, 2)
+            xevict(0, 2, "s")
+            trans(0, 3)
+            xevict(0, 3, "s")
+            lhuc_spread(1)
+            winter(0, 0, "v", 2)
+            xquant(0, 0)
+            winter(0, 1, "v", 2)
             for q in range(Q):
-                winter(4, q, "v", 2)
+                wquant(0, q, 2)
+            xquant(0, 1)
+            sigm(0, 1, G)
+            s1(0, 0, 0)
+            xsort(1, 0, "v")
+            xsort(1, 1, "v")
+            xquant(0, 2)
+            xquant(0, 3)
+            hevict(0, 0, 0)
+            sigm(1, 0, 2)
+            sorts = {2: "v-", 3: "--", 4: "v-", 5: "vv", 6: "vv"}
+            fill = {2: 0, 3: 0, 4: 0, 5: 2, 6: 1, 7: 3}
+            passes = [(g, n) for g in range(2) for n in range(NS)]
+            for k in range(2, 2 * G):
+                g, u = divmod(k, 2)
+                trans(g, 2 * u)
+                xevict(g, 2 * u, "s")
+                trans(g, 2 * u + 1)
+                xevict(g, 2 * u + 1, "s")
+                s1((k - 1) // 2, 0, (k - 1) % 2)
+                if u == 1:
+                    hjoin(g - 1, 0, "s")
+                elif k > 2:
+                    hquant(g - 2, 0)
+                if k == 4:
+                    sigm(1, 2, G)
+                if k == 6:
+                    winter(2, 0, "s", 2)
+                if k == 7:
+                    winter(2, 1, "v", 2)
+                    wquant(2, 0, 2)
+                if k + 1 < 2 * G:
+                    for j, eng in enumerate(sorts[k]):
+                        if eng != "-":
+                            xsort((k + 1) // 2, 2 * ((k + 1) % 2) + j, eng)
+                if k == 2:
+                    xsort(2, 0, "v")
+                for j in range(fill[k]):
+                    pg, pn = passes.pop(0)
+                    s2row(0, pg, [pn])
+                xquant(g, 2 * u)
+                xquant(g, 2 * u + 1)
+                hevict((k - 1) // 2, 0, (k - 1) % 2)
+            zbanks.extend([0, 1])
+            obanks.append(2)
+            for pg, pn in passes:
+                s2row(0, pg, [pn])
+            s2row(1, 0, [0])
+            s2row(1, 1, [0])
+            wquant(2, 1, 2)
+            s1(G - 1, 0, 1)
+            hquant(G - 2, 0)
+            hevict(G - 1, 0, 1)
+            hjoin(G - 1, 0, "s")
+            stage(0, 1)
+            s2row(0, 2, [0, 1, 2])
+            s2row(1, 2, [0])
+            s1(0, 1, 1)
+            hquant(G - 1, 0)
+            hevict(0, 1, 1)
+            hjoin(0, 1, "s")
             for n in range(NS):
-                s2(0, 512 * n, 512 * (n + 1), [3])
+                s2row(0, 3, [n])
                 finish(0, n)
-            k = 3
-            for n in range(NS):
-                for j in range(2 if n < 2 else 1):
-                    stage(k, 1)
-                    k += 1
-                s2(1, 512 * n, 512 * (n + 1), range(G))
-                finish(1, n)
-                if n < Q:
-                    wquant(4, n, 2)
-                if n >= 1:
-                    sigm(2, 2 * n - 2, 2 * n)
+            stage(2, 1)
+            s2row(1, 3, [0])
+            finish(1, 0)
+            stage(3, 1)
+            stage(4, 1)
+            winter(4, 0, "s", 2)
+            s2(1, 512, 1024, range(G))
+            finish(1, 1)
+            stage(5, 1)
+            stage(6, 1)
+            winter(4, 1, "s", 2)
+            s2row(2, 0, [0, 1])
+            wquant(4, 0, 2)
+            stage(7, 1)
+            s2(1, 1024, 1536, range(G))
+            finish(1, 2)
+            sigm(2, 0, 2)
+            wquant(4, 1, 2)
             hquant(G - 1, 1)
+            s2row(2, 0, [2])
+            for g in range(1, G - 1):
+                s2row(2, g, [0, 1, 2])
+            sigm(2, 2, G)
             share = [1, 2, 2, 2, 1, 0]
             for c in range(1, NC):
                 k = 0
@@ -349,7 +423,7 @@ def tile_lhuc_senone_gradient_s13_kernel(tc, x, w, lhuc, err_words, err_scales, 
                         hquant(G - 1, c + 1)
                     if h == NH - 1:
                         break
-                    s2(h, 512 * n, 512 * (n + 1), range(G))
+                    s2(h, 512 * n, 512 * (n + 1), [G - 1] if h == 2 else range(G))
                     finish(h, n)
                     if c + 2 < NC:
                         if i in (1, 2):

@@ -89,11 +89,9 @@ def tile_lhuc_senone_gradient_s13_kernel(tc, x, w, lhuc, err_words, err_scales, 
                 )
 
         def load_esca():
-            for k in range(4):
-                nc.sync.dma_start(
-                    out=esca[32 * k : 32 * k + 4, :, :].bitcast(I32),
-                    in_=err_scales[:, 4 * k : 4 * (k + 1), :].rearrange("g r n -> r g n").bitcast(I32),
-                )
+            rows = err_scales.rearrange("g (k r) n -> r k g n", r=4)
+            for r in range(4):
+                nc.sync.dma_start(out=esca[r:P:32, :, :].bitcast(I32), in_=rows[r].bitcast(I32))
 
         def load_ewor(g):
             nc.sync.dma_start(out=ewor[g][:].bitcast(I32), in_=err_words[g].bitcast(I32))
@@ -105,8 +103,8 @@ def tile_lhuc_senone_gradient_s13_kernel(tc, x, w, lhuc, err_words, err_scales, 
             xo = work.tile([P, 512], F32, name="xo", tag="xo", bufs=4)
             copy_on(
                 eng,
-                xo[:].rearrange("p (q u m) -> p q u m", q=Q, u=2),
-                xraw[g, t].bitcast(F32).rearrange("p (q m u) -> p q u m", q=Q, u=2),
+                xo[:].rearrange("p (q u m) -> p q m u", q=Q, u=2),
+                xraw[g, t].bitcast(F32).rearrange("p (q m u) -> p q m u", q=Q, u=2),
             )
             xord[g, t] = xo
 
@@ -273,12 +271,12 @@ def tile_lhuc_senone_gradient_s13_kernel(tc, x, w, lhuc, err_words, err_scales, 
             load_x(1, 2, 4)
             load_x(2, 0, 2)
             load_x(2, 2, 4)
-            load_esca()
-            load_ewor(0)
             load_x(3, 0, 2)
             load_x(3, 2, 4)
-            load_ewor(1)
+            load_esca()
+            load_ewor(0)
             load_w(1)
+            load_ewor(1)
             for g in range(2, G):
                 load_ewor(g)
             for c in (2, 3):
@@ -334,7 +332,7 @@ def tile_lhuc_senone_gradient_s13_kernel(tc, x, w, lhuc, err_words, err_scales, 
             hevict(0, 0, 0)
             sigm(1, 0, 2)
             sorts = {2: "v-", 3: "--", 4: "v-", 5: "vv", 6: "vv"}
-            fill = {2: 0, 3: 0, 4: 0, 5: 2, 6: 1, 7: 3}
+            fill = {2: 0, 3: 0, 4: 0, 5: 0, 6: 3, 7: 3}
             passes = [(g, n) for g in range(2) for n in range(NS)]
             for k in range(2, 2 * G):
                 g, u = divmod(k, 2)

@@ -39,11 +39,11 @@ def tile_lhuc_senone_gradient_s13_kernel(tc, x, w, lhuc, err_words, err_scales, 
         lcol = keep.tile([P, SPK, NC], F32, name="lcol")
         lraw = [keep.tile([P, G, WC], BF16, name="lraw%d" % c) for c in range(2)]
         amp = [keep.tile([P, G, WC], F32, name="amp%d" % c) for c in range(NC)]
-        xcod = [keep.tile([P, 4, Q * P], U32, name="xcod%d" % g, align_bytes=64) for g in range(G)]
-        xsca = [keep.tile([P, 4, Q * P], U8, name="xsca%d" % g, align_bytes=64) for g in range(G)]
+        xcod = [keep.tile([P, 4 * Q * P], U32, name="xcod%d" % g, align_bytes=64) for g in range(G)]
+        xsca = [keep.tile([P, 4 * Q * P], U8, name="xsca%d" % g, align_bytes=64) for g in range(G)]
         wraw = [[keep.tile([P, 4, WC], BF16, name="wraw%d_%d" % (c, q)) for q in range(Q)] for c in range(NC)]
-        wcod = [[keep.tile([P, WC], U32, name="wcod%d_%d" % (c, q), align_bytes=64) for q in range(Q)] for c in range(NC)]
-        wsca = [[keep.tile([P, WC], U8, name="wsca%d_%d" % (c, q), align_bytes=64) for q in range(Q)] for c in range(NC)]
+        wcod = [keep.tile([P, Q * WC], U32, name="wcod%d" % c, align_bytes=64) for c in range(NC)]
+        wsca = [keep.tile([P, Q * WC], U8, name="wsca%d" % c, align_bytes=64) for c in range(NC)]
         hcod = [keep.tile([P, G, WC], U32, name="hcod%d" % c, align_bytes=64) for c in range(NC)]
         hsca = [keep.tile([P, G, WC], U8, name="hsca%d" % c, align_bytes=64) for c in range(NC)]
         ewor = [keep.tile([P, 2 * S], U8, name="ewor%d" % g, align_bytes=64) for g in range(G)]
@@ -65,6 +65,7 @@ def tile_lhuc_senone_gradient_s13_kernel(tc, x, w, lhuc, err_words, err_scales, 
                 nc.vector.tensor_copy(out=dst, in_=src)
 
         xraw = {}
+        xrun = {}
 
         def load_x(g, a, b):
             xt = keep.tile([P, (b - a) * D], BF16, name="xraw%d_%d" % (g, a))
@@ -72,6 +73,8 @@ def tile_lhuc_senone_gradient_s13_kernel(tc, x, w, lhuc, err_words, err_scales, 
             nc.sync.dma_start(out=xt[:], in_=rows[:, a * D : b * D])
             for t in range(a, b):
                 xraw[g, t] = xt[:, (t - a) * D : (t - a + 1) * D]
+                xrun[g, t, t + 1] = xraw[g, t]
+            xrun[g, a, b] = xt[:]
 
         def load_w(c):
             for q in range(Q):
@@ -99,14 +102,14 @@ def tile_lhuc_senone_gradient_s13_kernel(tc, x, w, lhuc, err_words, err_scales, 
         xgrp = {}
         xord = {}
 
-        def xsort(g, t, eng):
-            xo = work.tile([P, 512], F32, name="xo", tag="xo", bufs=4)
-            copy_on(
-                eng,
-                xo[:].rearrange("p (q u m) -> p q m u", q=Q, u=2),
-                xraw[g, t].bitcast(F32).rearrange("p (q m u) -> p q m u", q=Q, u=2),
+        def xsort(g, lo, hi):
+            xo = work.tile([P, (hi - lo) * 512], F32, name="xo", tag="xo", bufs=3)
+            nc.vector.tensor_copy(
+                out=xo[:].rearrange("p (a u m) -> p a m u", u=2, m=P),
+                in_=xrun[g, lo, hi].bitcast(F32).rearrange("p (a m u) -> p a m u", u=2, m=P),
             )
-            xord[g, t] = xo
+            for t in range(lo, hi):
+                xord[g, t] = xo[:, 512 * (t - lo) : 512 * (t - lo + 1)]
 
         def trans(g, t):
             b = bank(xbanks[count["x"] % len(xbanks)], [P, 512], F32)
@@ -133,31 +136,29 @@ def tile_lhuc_senone_gradient_s13_kernel(tc, x, w, lhuc, err_words, err_scales, 
                 xbank[g, t][:].rearrange("p (q u m) -> p q m u", q=Q, u=2),
             )
 
-        def xquant(g, t):
+        def xquant(g, lo, hi):
             nc.vector.quantize_mx(
-                out=xcod[g][:, t, :].bitcast(FP8X4),
-                scales=xsca[g][:, t, :],
-                in_=xgrp[g, t // 2][:, D * (t % 2) : D * (t % 2 + 1)],
+                out=xcod[g][:, Q * P * lo : Q * P * hi].bitcast(FP8X4),
+                scales=xsca[g][:, Q * P * lo : Q * P * hi],
+                in_=xgrp[g, lo // 2][:, D * (lo % 2) : D * (lo % 2 + hi - lo)],
             )
 
         wgrp = {}
 
-        def winter(h, q, eng, n):
-            c, off = divmod(P * h, WC)
-            wg = work.tile([P, P * n, 4], BF16, name="wg", tag="wg", align_bytes=64)
+        def winter(c, q, eng):
+            if c not in wgrp:
+                wgrp[c] = work.tile([P, Q * WC * 4], BF16, name="wg", tag="wg", bufs=2, align_bytes=64)
             copy_on(
                 eng,
-                wg[:].rearrange("p (c i) j -> p c j i", i=4),
-                wraw[c][q][:, :, off : off + P * n].rearrange("p j (c i) -> p c j i", i=4),
+                wgrp[c][:, 4 * WC * q : 4 * WC * (q + 1)].rearrange("p (c i j) -> p c j i", i=4, j=4),
+                wraw[c][q][:].rearrange("p j (c i) -> p c j i", i=4),
             )
-            wgrp[h, q] = wg
 
-        def wquant(h, q, n):
-            c, off = divmod(P * h, WC)
+        def wquant(c, lo, hi):
             nc.vector.quantize_mx(
-                out=wcod[c][q][:, off : off + P * n].bitcast(FP8X4),
-                scales=wsca[c][q][:, off : off + P * n],
-                in_=wgrp[h, q][:].rearrange("p n j -> p (n j)"),
+                out=wcod[c][:, WC * lo : WC * hi].bitcast(FP8X4),
+                scales=wsca[c][:, WC * lo : WC * hi],
+                in_=wgrp[c][:, 4 * WC * lo : 4 * WC * hi],
             )
 
         abank = {}
@@ -197,10 +198,10 @@ def tile_lhuc_senone_gradient_s13_kernel(tc, x, w, lhuc, err_words, err_scales, 
                 for q in range(Q):
                     nc.tensor.matmul_mx(
                         out=z[:, e, :],
-                        lhsT=xcod[g][:, t, P * q : P * (q + 1)].bitcast(FP8X4),
-                        lhsT_scale=xsca[g][:, t, P * q : P * (q + 1)],
-                        rhs=wcod[c][q][:].bitcast(FP8X4),
-                        rhs_scale=wsca[c][q][:],
+                        lhsT=xcod[g][:, P * (Q * t + q) : P * (Q * t + q + 1)].bitcast(FP8X4),
+                        lhsT_scale=xsca[g][:, P * (Q * t + q) : P * (Q * t + q + 1)],
+                        rhs=wcod[c][:, WC * q : WC * (q + 1)].bitcast(FP8X4),
+                        rhs_scale=wsca[c][:, WC * q : WC * (q + 1)],
                         start=(q == 0),
                         stop=(q == Q - 1),
                     )
@@ -264,24 +265,23 @@ def tile_lhuc_senone_gradient_s13_kernel(tc, x, w, lhuc, err_words, err_scales, 
             nc.vector.memset(lrow[64:128, :], 0.0)
             make_identity(nc, ident[:])
             nc.vector.memset(esca[:].rearrange("p g n -> p (g n)").bitcast(I32), 0)
-            for t in range(4):
-                load_x(0, t, t + 1)
+            load_x(0, 0, 1)
+            load_x(0, 1, 2)
             load_w(0)
-            load_x(1, 0, 2)
-            load_x(1, 2, 4)
-            load_x(2, 0, 2)
-            load_x(2, 2, 4)
-            load_x(3, 0, 2)
-            load_x(3, 2, 4)
+            load_x(0, 2, 3)
+            load_x(0, 3, 4)
+            for g in range(1, G):
+                load_x(g, 0, 2)
+                load_x(g, 2, 4)
             load_esca()
             load_ewor(0)
             load_w(1)
-            load_ewor(1)
-            for g in range(2, G):
+            for g in range(1, G):
                 load_ewor(g)
-            for c in (2, 3):
-                load_w(c)
-                load_lhuc_spread(c)
+            load_w(2)
+            load_w(3)
+            load_lhuc_spread(2)
+            load_lhuc_spread(3)
 
             def stage(k, c):
                 g, u = divmod(k, 2)
@@ -303,37 +303,30 @@ def tile_lhuc_senone_gradient_s13_kernel(tc, x, w, lhuc, err_words, err_scales, 
             lhuc_turn()
             lhuc_repeat(0)
             trans(0, 0)
-            xsort(0, 1, "v")
+            lhuc_repeat(1)
+            xevict(0, 0, "v")
+            trans(0, 1)
             lhuc_spread(0)
             sigm(0, 0, 1)
-            xevict(0, 0, "s")
-            xsort(0, 2, "v")
-            lhuc_repeat(1)
-            trans(0, 1)
-            xsort(0, 3, "v")
             xevict(0, 1, "s")
+            sigm(0, 1, G)
+            lhuc_spread(1)
+            winter(0, 0, "v")
+            xquant(0, 0, 1)
+            winter(0, 1, "v")
             trans(0, 2)
             xevict(0, 2, "s")
+            wquant(0, 0, 1)
+            wquant(0, 1, 2)
+            xquant(0, 1, 2)
             trans(0, 3)
             xevict(0, 3, "s")
-            lhuc_spread(1)
-            winter(0, 0, "v", 2)
-            xquant(0, 0)
-            winter(0, 1, "v", 2)
-            for q in range(Q):
-                wquant(0, q, 2)
-            xquant(0, 1)
-            sigm(0, 1, G)
-            s1(0, 0, 0)
-            xsort(1, 0, "v")
-            xsort(1, 1, "v")
-            xquant(0, 2)
-            xquant(0, 3)
-            hevict(0, 0, 0)
             sigm(1, 0, 2)
-            sorts = {2: "v-", 3: "--", 4: "v-", 5: "vv", 6: "vv"}
-            fill = {2: 0, 3: 0, 4: 0, 5: 0, 6: 3, 7: 3}
-            passes = [(g, n) for g in range(2) for n in range(NS)]
+            s1(0, 0, 0)
+            xsort(1, 0, 2)
+            xquant(0, 2, 4)
+            hevict(0, 0, 0)
+            sorts = {2: [(1, 2, 3), (2, 0, 1)], 4: [(3, 0, 2)], 5: [(3, 2, 4)]}
             for k in range(2, 2 * G):
                 g, u = divmod(k, 2)
                 trans(g, 2 * u)
@@ -347,67 +340,67 @@ def tile_lhuc_senone_gradient_s13_kernel(tc, x, w, lhuc, err_words, err_scales, 
                     hquant(g - 2, 0)
                 if k == 4:
                     sigm(1, 2, G)
-                if k == 6:
-                    winter(2, 0, "s", 2)
-                if k == 7:
-                    winter(2, 1, "v", 2)
-                    wquant(2, 0, 2)
-                if k + 1 < 2 * G:
-                    for j, eng in enumerate(sorts[k]):
-                        if eng != "-":
-                            xsort((k + 1) // 2, 2 * ((k + 1) % 2) + j, eng)
                 if k == 2:
-                    xsort(2, 0, "v")
-                for j in range(fill[k]):
-                    pg, pn = passes.pop(0)
-                    s2row(0, pg, [pn])
-                xquant(g, 2 * u)
-                xquant(g, 2 * u + 1)
+                    for run in sorts[k]:
+                        xsort(*run)
+                if k >= 6:
+                    s2row(0, k - 6, [0, 1, 2])
+                xquant(g, 2 * u, 2 * u + 1)
+                xquant(g, 2 * u + 1, 2 * u + 2)
+                if k > 2:
+                    for run in sorts.get(k, []):
+                        xsort(*run)
                 hevict((k - 1) // 2, 0, (k - 1) % 2)
-            zbanks.extend([0, 1])
-            obanks.append(2)
-            for pg, pn in passes:
-                s2row(0, pg, [pn])
+                if k == 6:
+                    winter(1, 0, "s")
+                    winter(1, 1, "v")
+            zbanks.append(0)
+            obanks.extend([2, 1])
             s2row(1, 0, [0])
             s2row(1, 1, [0])
-            wquant(2, 1, 2)
-            s1(G - 1, 0, 1)
             hquant(G - 2, 0)
+            s1(G - 1, 0, 1)
             hevict(G - 1, 0, 1)
             hjoin(G - 1, 0, "s")
-            stage(0, 1)
+            wquant(1, 0, 2)
+            winter(2, 0, "s")
+            winter(2, 1, "s")
+            s2row(1, 0, [1])
+            s2row(1, 1, [1])
             s2row(0, 2, [0, 1, 2])
-            s2row(1, 2, [0])
-            s1(0, 1, 1)
+            s2row(1, 2, [0, 1])
+            s1(0, 1, 0)
             hquant(G - 1, 0)
-            hevict(0, 1, 1)
-            hjoin(0, 1, "s")
+            hevict(0, 1, 0)
+            stage(1, 1)
             for n in range(NS):
                 s2row(0, 3, [n])
                 finish(0, n)
             stage(2, 1)
-            s2row(1, 3, [0])
-            finish(1, 0)
             stage(3, 1)
+            for n in range(2):
+                s2row(1, 3, [n])
+                finish(1, n)
             stage(4, 1)
-            winter(4, 0, "s", 2)
-            s2(1, 512, 1024, range(G))
-            finish(1, 1)
+            wquant(2, 0, 2)
             stage(5, 1)
-            stage(6, 1)
-            winter(4, 1, "s", 2)
-            s2row(2, 0, [0, 1])
-            wquant(4, 0, 2)
-            stage(7, 1)
             s2(1, 1024, 1536, range(G))
             finish(1, 2)
             sigm(2, 0, 2)
-            wquant(4, 1, 2)
-            hquant(G - 1, 1)
-            s2row(2, 0, [2])
-            for g in range(1, G - 1):
-                s2row(2, g, [0, 1, 2])
+            stage(6, 1)
+            winter(3, 0, "v")
+            s2row(2, 0, [0, 1, 2])
+            stage(7, 1)
             sigm(2, 2, G)
+            s2row(2, 1, [0, 1, 2])
+            s2row(3, 0, [0])
+            s2row(3, 1, [0])
+            hquant(G - 1, 1)
+            winter(3, 1, "v")
+            s2row(2, 2, [0, 1, 2])
+            s2row(3, 2, [0])
+            sigm(3, 0, 2)
+            wquant(3, 0, 2)
             share = [1, 2, 2, 2, 1, 0]
             for c in range(1, NC):
                 k = 0
@@ -421,15 +414,11 @@ def tile_lhuc_senone_gradient_s13_kernel(tc, x, w, lhuc, err_words, err_scales, 
                         hquant(G - 1, c + 1)
                     if h == NH - 1:
                         break
-                    s2(h, 512 * n, 512 * (n + 1), [G - 1] if h == 2 else range(G))
+                    s2(h, 512 * n, 512 * (n + 1), [G - 1] if c == 1 and i < 4 else range(G))
                     finish(h, n)
                     if c + 2 < NC:
-                        if i in (1, 2):
-                            winter(2 * c + 4, i - 1, "v", 2)
-                        if i in (3, 4):
-                            wquant(2 * c + 4, i - 3, 2)
-                        if i == 4:
-                            sigm(c + 2, 0, G)
+                        if i == 0:
+                            sigm(c + 2, 2, G)
             cuts = [0, 512, 768, 1024, 1280, 1408, S]
             for i in range(len(cuts) - 1):
                 s2(NH - 1, cuts[i], cuts[i + 1], range(G))

@@ -47,7 +47,7 @@ def tile_lhuc_senone_gradient_s13_kernel(tc, x, w, lhuc, err_words, err_scales, 
         hcod = [keep.tile([P, G, WC], U32, name="hcod%d" % c, align_bytes=64) for c in range(NC)]
         hsca = [keep.tile([P, G, WC], U8, name="hsca%d" % c, align_bytes=64) for c in range(NC)]
         ewor = [keep.tile([P, 2 * S], U8, name="ewor%d" % g, align_bytes=64) for g in range(G)]
-        esca = keep.tile([P, G, S], U8, name="esca", align_bytes=64)
+        esca = [keep.tile([P, 2, S], U8, name="esca%d" % a, align_bytes=64) for a in range(G // 2)]
 
         def bank(i, shape, dtype):
             b = psum.tile(shape, dtype, name="bank%d" % i, tag="bank%d" % i)
@@ -73,8 +73,8 @@ def tile_lhuc_senone_gradient_s13_kernel(tc, x, w, lhuc, err_words, err_scales, 
             nc.sync.dma_start(out=xt[:], in_=rows[:, a * D : b * D])
             for t in range(a, b):
                 xraw[g, t] = xt[:, (t - a) * D : (t - a + 1) * D]
-                xrun[g, t, t + 1] = xraw[g, t]
-            xrun[g, a, b] = xt[:]
+                for end in range(t + 1, b + 1):
+                    xrun[g, t, end] = xt[:, (t - a) * D : (end - a) * D]
 
         def load_w(c):
             for q in range(Q):
@@ -91,10 +91,10 @@ def tile_lhuc_senone_gradient_s13_kernel(tc, x, w, lhuc, err_words, err_scales, 
                     in_=rows[s, :, WC * c : WC * (c + 1)].partition_broadcast(64),
                 )
 
-        def load_esca():
+        def load_esca(a):
             rows = err_scales.rearrange("g (k r) n -> r k g n", r=4)
             for r in range(4):
-                nc.sync.dma_start(out=esca[r:P:32, :, :].bitcast(I32), in_=rows[r].bitcast(I32))
+                nc.sync.dma_start(out=esca[a][r:P:32, :, :].bitcast(I32), in_=rows[r, :, 2 * a : 2 * a + 2, :].bitcast(I32))
 
         def load_ewor(g):
             nc.sync.dma_start(out=ewor[g][:].bitcast(I32), in_=err_words[g].bitcast(I32))
@@ -242,7 +242,7 @@ def tile_lhuc_senone_gradient_s13_kernel(tc, x, w, lhuc, err_words, err_scales, 
                     lhsT=hcod[h // 2][:, g, P * (h % 2) : P * (h % 2 + 1)].bitcast(FP8X4),
                     lhsT_scale=hsca[h // 2][:, g, P * (h % 2) : P * (h % 2 + 1)],
                     rhs=ewor[g][:, 2 * lo : 2 * hi].bitcast(FP4X4),
-                    rhs_scale=esca[:, g, lo:hi],
+                    rhs_scale=esca[g // 2][:, g % 2, lo:hi],
                     start=(g == 0),
                     stop=(g == G - 1),
                 )
@@ -264,20 +264,25 @@ def tile_lhuc_senone_gradient_s13_kernel(tc, x, w, lhuc, err_words, err_scales, 
             nc.vector.memset(lrow[32:64, :], 0.0)
             nc.vector.memset(lrow[64:128, :], 0.0)
             make_identity(nc, ident[:])
-            nc.vector.memset(esca[:].rearrange("p g n -> p (g n)").bitcast(I32), 0)
+            for plane in esca:
+                nc.vector.memset(plane[:].rearrange("p g n -> p (g n)").bitcast(I32), 0)
             load_x(0, 0, 1)
             load_x(0, 1, 2)
             load_w(0)
             load_x(0, 2, 3)
             load_x(0, 3, 4)
-            for g in range(1, G):
-                load_x(g, 0, 2)
-                load_x(g, 2, 4)
-            load_esca()
+            load_x(1, 0, 2)
+            load_x(1, 2, 4)
+            load_x(2, 0, 2)
+            load_x(2, 2, 4)
+            load_x(3, 0, 4)
+            load_esca(0)
             load_ewor(0)
             load_w(1)
-            for g in range(1, G):
-                load_ewor(g)
+            load_ewor(1)
+            load_esca(1)
+            load_ewor(2)
+            load_ewor(3)
             load_w(2)
             load_w(3)
             load_lhuc_spread(2)
@@ -326,7 +331,8 @@ def tile_lhuc_senone_gradient_s13_kernel(tc, x, w, lhuc, err_words, err_scales, 
             xsort(1, 0, 2)
             xquant(0, 2, 4)
             hevict(0, 0, 0)
-            sorts = {2: [(1, 2, 3), (2, 0, 1)], 4: [(3, 0, 2)], 5: [(3, 2, 4)]}
+            xsort(1, 2, 3)
+            sorts = {2: [(2, 0, 1)], 4: [(3, 0, 2)], 5: [(3, 2, 4)]}
             for k in range(2, 2 * G):
                 g, u = divmod(k, 2)
                 trans(g, 2 * u)
@@ -340,16 +346,12 @@ def tile_lhuc_senone_gradient_s13_kernel(tc, x, w, lhuc, err_words, err_scales, 
                     hquant(g - 2, 0)
                 if k == 4:
                     sigm(1, 2, G)
-                if k == 2:
-                    for run in sorts[k]:
-                        xsort(*run)
                 if k >= 6:
                     s2row(0, k - 6, [0, 1, 2])
                 xquant(g, 2 * u, 2 * u + 1)
                 xquant(g, 2 * u + 1, 2 * u + 2)
-                if k > 2:
-                    for run in sorts.get(k, []):
-                        xsort(*run)
+                for run in sorts.get(k, []):
+                    xsort(*run)
                 hevict((k - 1) // 2, 0, (k - 1) % 2)
                 if k == 6:
                     winter(1, 0, "s")
@@ -399,7 +401,6 @@ def tile_lhuc_senone_gradient_s13_kernel(tc, x, w, lhuc, err_words, err_scales, 
             winter(3, 1, "v")
             s2row(2, 2, [0, 1, 2])
             s2row(3, 2, [0])
-            sigm(3, 0, 2)
             wquant(3, 0, 2)
             share = [1, 2, 2, 2, 1, 0]
             for c in range(1, NC):
@@ -417,8 +418,8 @@ def tile_lhuc_senone_gradient_s13_kernel(tc, x, w, lhuc, err_words, err_scales, 
                     s2(h, 512 * n, 512 * (n + 1), [G - 1] if c == 1 and i < 4 else range(G))
                     finish(h, n)
                     if c + 2 < NC:
-                        if i == 0:
-                            sigm(c + 2, 2, G)
+                        if i in (2, 4):
+                            sigm(c + 2, i - 2, i)
             cuts = [0, 512, 768, 1024, 1280, 1408, S]
             for i in range(len(cuts) - 1):
                 s2(NH - 1, cuts[i], cuts[i + 1], range(G))

@@ -49,14 +49,16 @@ def tile_lhuc_senone_gradient_s13_kernel(tc, x, w, lhuc, err_words, err_scales, 
         ewor = [keep.tile([P, 2 * S], U8, name="ewor%d" % g, align_bytes=64) for g in range(G)]
         esca = [keep.tile([P, 2, S], U8, name="esca%d" % a, align_bytes=64) for a in range(G // 2)]
 
-        def bank(i, shape, dtype):
-            b = psum.tile(shape, dtype, name="bank%d" % i, tag="bank%d" % i)
+        free = list(range(8))
+        held = {}
+
+        def take(user, shape):
+            held[user] = free.pop(0)
+            b = psum.tile(shape, F32, name="bank%d" % held[user], tag="bank%d" % held[user])
             return b
 
-        xbanks = [0, 1, 2]
-        zbanks = [4, 7]
-        obanks = [3, 5, 6]
-        count = {"x": 0, "z": 0, "o": 0}
+        def give(user):
+            free.append(held.pop(user))
 
         def copy_on(eng, dst, src):
             if eng == "s":
@@ -76,8 +78,8 @@ def tile_lhuc_senone_gradient_s13_kernel(tc, x, w, lhuc, err_words, err_scales, 
                 for end in range(t + 1, b + 1):
                     xrun[g, t, end] = xt[:, (t - a) * D : (end - a) * D]
 
-        def load_w(c):
-            for q in range(Q):
+        def load_w(c, passes=range(Q)):
+            for q in passes:
                 nc.sync.dma_start(
                     out=wraw[c][q][:],
                     in_=w[512 * q : 512 * (q + 1), WC * c : WC * (c + 1)].rearrange("(p j) n -> p j n", j=4),
@@ -112,8 +114,7 @@ def tile_lhuc_senone_gradient_s13_kernel(tc, x, w, lhuc, err_words, err_scales, 
                 xord[g, t] = xo[:, 512 * (t - lo) : 512 * (t - lo + 1)]
 
         def trans(g, t):
-            b = bank(xbanks[count["x"] % len(xbanks)], [P, 512], F32)
-            count["x"] += 1
+            b = take(("x", g, t), [P, 512])
             words = xraw[g, t].bitcast(F32)
             for q in range(Q):
                 for u in range(2):
@@ -135,6 +136,7 @@ def tile_lhuc_senone_gradient_s13_kernel(tc, x, w, lhuc, err_words, err_scales, 
                 xgrp[g, t // 2][:, D * (t % 2) : D * (t % 2 + 1)].bitcast(F32).rearrange("p (q m u) -> p q m u", q=Q, u=2),
                 xbank[g, t][:].rearrange("p (q u m) -> p q m u", q=Q, u=2),
             )
+            give(("x", g, t))
 
         def xquant(g, lo, hi):
             nc.vector.quantize_mx(
@@ -164,15 +166,16 @@ def tile_lhuc_senone_gradient_s13_kernel(tc, x, w, lhuc, err_words, err_scales, 
         abank = {}
 
         def lhuc_turn():
-            b = bank(7, [P, P], F32)
+            b = take("turn", [P, P])
             nc.tensor.transpose(b[:], lrow[:].bitcast(F32), ident[:])
             nc.vector.tensor_copy(out=lcol[:].rearrange("p s c -> p (s c)"), in_=b[:, 0 : SPK * NC])
+            give("turn")
 
         def lhuc_repeat(c):
             nc.vector.tensor_copy(out=lrep[c][:], in_=lcol[:, :, c : c + 1].to_broadcast([P, SPK, 64]))
 
         def lhuc_spread(c):
-            b = bank(5 + c, [P, G, P], F32)
+            b = take(("amp", c), [P, G, P])
             for g in range(G):
                 nc.tensor.transpose(b[:, g, :], lrep[c][:, 2 * g : 2 * g + 2, :].rearrange("p s r -> p (s r)"), ident[:])
             abank[c] = b
@@ -183,29 +186,30 @@ def tile_lhuc_senone_gradient_s13_kernel(tc, x, w, lhuc, err_words, err_scales, 
             else:
                 src = lraw[c - 2][:, lo:hi, :]
             nc.scalar.activation(out=amp[c][:, lo:hi, :], in_=src, func=ACT.Sigmoid)
+            if c < 2 and hi == G:
+                give(("amp", c))
 
         halves = {}
         zb = {}
         hgrp = {}
 
-        def s1(g, c, u):
-            if u == 0:
-                halves[g, c] = work.tile([P, 2, WC, 2], BF16, name="half", tag="half", bufs=3, align_bytes=64)
-            z = bank(zbanks[count["z"] % len(zbanks)], [P, 2, WC], F32)
-            count["z"] += 1
-            for e in range(2):
-                t = 2 * u + e
-                for q in range(Q):
+        def s1(g, c, u, passes=range(Q)):
+            if passes[0] == 0:
+                if u == 0:
+                    halves[g, c] = work.tile([P, 2, WC, 2], BF16, name="half", tag="half", bufs=3, align_bytes=64)
+                zb[g, c, u] = take(("z", g, c, u), [P, 2, WC])
+            for q in passes:
+                for e in range(2):
+                    t = 2 * u + e
                     nc.tensor.matmul_mx(
-                        out=z[:, e, :],
+                        out=zb[g, c, u][:, e, :],
                         lhsT=xcod[g][:, P * (Q * t + q) : P * (Q * t + q + 1)].bitcast(FP8X4),
                         lhsT_scale=xsca[g][:, P * (Q * t + q) : P * (Q * t + q + 1)],
                         rhs=wcod[c][:, WC * q : WC * (q + 1)].bitcast(FP8X4),
                         rhs_scale=wsca[c][:, WC * q : WC * (q + 1)],
-                        start=(q == 0),
-                        stop=(q == Q - 1),
+                        start=(q == 0 and e == 0),
+                        stop=(q == Q - 1 and e == 1),
                     )
-            zb[g, c, u] = z
 
         def hevict(g, c, u):
             nc.vector.scalar_tensor_tensor(
@@ -216,6 +220,7 @@ def tile_lhuc_senone_gradient_s13_kernel(tc, x, w, lhuc, err_words, err_scales, 
                 op0=ALU.max,
                 op1=ALU.mult,
             )
+            give(("z", g, c, u))
 
         def hjoin(g, c, eng):
             hg = work.tile([P, WC * 4], BF16, name="hg", tag="hg", bufs=3, align_bytes=64)
@@ -227,15 +232,14 @@ def tile_lhuc_senone_gradient_s13_kernel(tc, x, w, lhuc, err_words, err_scales, 
             hgrp[g, c] = hg
 
         def hquant(g, c):
-            nc.vector.quantize_mx(out=hcod[c][:, g, :].bitcast(FP8X4), scales=hsca[c][:, g, :], in_=hgrp[g, c][:])
+            nc.vector.quantize_mx(out=hcod[c][:, g, :].bitcast(FP8X4), scales=hsca[c][:, g, :], in_=hgrp.pop((g, c))[:])
 
         ob = {}
         og = {}
 
         def s2(h, lo, hi, groups):
             if groups[0] == 0:
-                ob[h, lo] = bank(obanks[count["o"] % len(obanks)], [P, hi - lo], F32)
-                count["o"] += 1
+                ob[h, lo] = take(("o", h, lo), [P, hi - lo])
             for g in groups:
                 nc.tensor.matmul_mx(
                     out=ob[h, lo][:],
@@ -255,6 +259,7 @@ def tile_lhuc_senone_gradient_s13_kernel(tc, x, w, lhuc, err_words, err_scales, 
                 nc.scalar.activation(out=dst, in_=ob[h, lo][:], func=ACT.Copy, scale=2.0)
             else:
                 nc.vector.tensor_scalar(out=dst, in0=ob[h, lo][:], scalar1=2.0, scalar2=None, op0=ALU.mult)
+            give(("o", h, lo))
 
         def store(h, lo, hi):
             nc.sync.dma_start(out=out[P * h : P * (h + 1), lo:hi], in_=og[h][:, lo:hi])
@@ -275,11 +280,12 @@ def tile_lhuc_senone_gradient_s13_kernel(tc, x, w, lhuc, err_words, err_scales, 
             load_x(1, 2, 4)
             load_x(2, 0, 2)
             load_x(2, 2, 4)
-            load_x(3, 0, 4)
+            load_x(3, 0, 2)
+            load_x(3, 2, 4)
             load_esca(0)
             load_ewor(0)
-            load_w(1)
             load_ewor(1)
+            load_w(1)
             load_esca(1)
             load_ewor(2)
             load_ewor(3)
@@ -294,7 +300,7 @@ def tile_lhuc_senone_gradient_s13_kernel(tc, x, w, lhuc, err_words, err_scales, 
                 hevict(g, c, u)
                 if u == 1:
                     hjoin(g, c, "s")
-                    if g > 0 and c > 0:
+                    if (g - 1, c) in hgrp:
                         hquant(g - 1, c)
 
             def finish(h, n):
@@ -327,46 +333,67 @@ def tile_lhuc_senone_gradient_s13_kernel(tc, x, w, lhuc, err_words, err_scales, 
             trans(0, 3)
             xevict(0, 3, "s")
             sigm(1, 0, 2)
+
+            def turn(g, lo, hi):
+                for t in range(lo, hi):
+                    trans(g, t)
+                    xevict(g, t, "s")
+
             s1(0, 0, 0)
-            xsort(1, 0, 2)
-            xquant(0, 2, 4)
+            xquant(0, 2, 3)
+            xsort(1, 1, 2)
+            xquant(0, 3, 4)
+            turn(1, 0, 2)
             hevict(0, 0, 0)
             xsort(1, 2, 3)
-            sorts = {2: [(2, 0, 1)], 4: [(3, 0, 2)], 5: [(3, 2, 4)]}
-            for k in range(2, 2 * G):
-                g, u = divmod(k, 2)
-                trans(g, 2 * u)
-                xevict(g, 2 * u, "s")
-                trans(g, 2 * u + 1)
-                xevict(g, 2 * u + 1, "s")
-                s1((k - 1) // 2, 0, (k - 1) % 2)
-                if u == 1:
-                    hjoin(g - 1, 0, "s")
-                elif k > 2:
-                    hquant(g - 2, 0)
-                if k == 4:
-                    sigm(1, 2, G)
-                if k >= 6:
-                    s2row(0, k - 6, [0, 1, 2])
-                xquant(g, 2 * u, 2 * u + 1)
-                xquant(g, 2 * u + 1, 2 * u + 2)
-                for run in sorts.get(k, []):
-                    xsort(*run)
-                hevict((k - 1) // 2, 0, (k - 1) % 2)
-                if k == 6:
-                    winter(1, 0, "s")
-                    winter(1, 1, "v")
-            zbanks.append(0)
-            obanks.extend([2, 1])
+            s1(0, 0, 1)
+            turn(1, 2, 4)
+            xquant(1, 0, 1)
+            xquant(1, 1, 2)
+            s1(1, 0, 0)
+            xsort(2, 0, 1)
+            hevict(0, 0, 1)
+            hjoin(0, 0, "s")
+            xquant(1, 2, 4)
+            turn(2, 0, 4)
+            hevict(1, 0, 0)
+            hquant(0, 0)
+            s1(1, 0, 1)
+            xquant(2, 0, 1)
+            xquant(2, 1, 2)
+            s1(2, 0, 0)
+            xsort(3, 0, 2)
+            xsort(3, 2, 4)
+            sigm(1, 2, G)
+            hevict(1, 0, 1)
+            xquant(2, 2, 4)
+            turn(3, 0, 2)
+            hjoin(1, 0, "s")
+            turn(3, 2, 4)
+            hevict(2, 0, 0)
+            s1(2, 0, 1)
+            s2row(0, 0, [0, 1])
+            xquant(3, 0, 1)
+            xquant(3, 1, 2)
+            hquant(1, 0)
+            s1(3, 0, 0)
+            hevict(2, 0, 1)
+            xquant(3, 2, 4)
+            hjoin(2, 0, "s")
+            winter(1, 0, "s")
+            hevict(3, 0, 0)
+            s2row(0, 1, [0, 1])
+            s2row(0, 0, [2])
+            s2row(0, 1, [2])
             s2row(1, 0, [0])
             s2row(1, 1, [0])
             hquant(G - 2, 0)
+            winter(1, 1, "v")
             s1(G - 1, 0, 1)
             hevict(G - 1, 0, 1)
             hjoin(G - 1, 0, "s")
             wquant(1, 0, 2)
             winter(2, 0, "s")
-            winter(2, 1, "s")
             s2row(1, 0, [1])
             s2row(1, 1, [1])
             s2row(0, 2, [0, 1, 2])
@@ -378,6 +405,7 @@ def tile_lhuc_senone_gradient_s13_kernel(tc, x, w, lhuc, err_words, err_scales, 
             for n in range(NS):
                 s2row(0, 3, [n])
                 finish(0, n)
+            winter(2, 1, "v")
             stage(2, 1)
             stage(3, 1)
             for n in range(2):
@@ -392,6 +420,7 @@ def tile_lhuc_senone_gradient_s13_kernel(tc, x, w, lhuc, err_words, err_scales, 
             stage(6, 1)
             winter(3, 0, "v")
             s2row(2, 0, [0, 1, 2])
+            hquant(2, 1)
             stage(7, 1)
             sigm(2, 2, G)
             s2row(2, 1, [0, 1, 2])

@@ -265,7 +265,7 @@ def tile_lhuc_senone_gradient_s13_kernel(tc, x, w, lhuc, err_words, err_scales, 
             nc.sync.dma_start(out=out[P * h : P * (h + 1), lo:hi], in_=og[h][:, lo:hi])
 
         with tc.manual_schedule():
-            nc.scalar.dma_start(out=lrow[0:32, :], in_=lhuc.rearrange("s (c n) -> (s c) n", n=WC))
+            nc.sync.dma_start(out=lrow[0:32, :], in_=lhuc.rearrange("s (c n) -> (s c) n", n=WC))
             nc.vector.memset(lrow[32:64, :], 0.0)
             nc.vector.memset(lrow[64:128, :], 0.0)
             make_identity(nc, ident[:])
@@ -353,20 +353,22 @@ def tile_lhuc_senone_gradient_s13_kernel(tc, x, w, lhuc, err_words, err_scales, 
             s1(1, 0, 0)
             xsort(2, 0, 1)
             hevict(0, 0, 1)
-            hjoin(0, 0, "s")
+            xsort(2, 3, 4)
             xquant(1, 2, 4)
-            turn(2, 0, 4)
+            turn(2, 0, 2)
+            hjoin(0, 0, "s")
+            turn(2, 2, 4)
             hevict(1, 0, 0)
-            hquant(0, 0)
             s1(1, 0, 1)
             xquant(2, 0, 1)
             xquant(2, 1, 2)
             s1(2, 0, 0)
             xsort(3, 0, 2)
-            xsort(3, 2, 4)
+            xsort(3, 2, 3)
             sigm(1, 2, G)
             hevict(1, 0, 1)
             xquant(2, 2, 4)
+            hquant(0, 0)
             turn(3, 0, 2)
             hjoin(1, 0, "s")
             turn(3, 2, 4)

@@ -35,10 +35,8 @@ def tile_lhuc_senone_gradient_s13_kernel(tc, x, w, lhuc, err_words, err_scales, 
 
         ident = keep.tile([P, P], F32, name="ident")
         lrow = keep.tile([P, WC], BF16, name="lrow", align_bytes=64)
-        lrep = [keep.tile([P, SPK, 64], F32, name="lrep%d" % c, align_bytes=64) for c in range(2)]
-        lcol = keep.tile([P, SPK, NC], F32, name="lcol")
-        lraw = [keep.tile([P, G, WC], BF16, name="lraw%d" % c) for c in range(2)]
-        amp = [keep.tile([P, G, WC], F32, name="amp%d" % c) for c in range(NC)]
+        lrep = keep.tile([P, NC, P], F32, name="lrep", align_bytes=64)
+        amp = keep.tile([P, H], F32, name="amp")
         xcod = [keep.tile([P, 4 * Q * P], U32, name="xcod%d" % g, align_bytes=64) for g in range(G)]
         xsca = [keep.tile([P, 4 * Q * P], U8, name="xsca%d" % g, align_bytes=64) for g in range(G)]
         wraw = [[keep.tile([P, 4, WC], BF16, name="wraw%d_%d" % (c, q)) for q in range(Q)] for c in range(NC)]
@@ -71,8 +69,8 @@ def tile_lhuc_senone_gradient_s13_kernel(tc, x, w, lhuc, err_words, err_scales, 
 
         def load_x(g, a, b):
             xt = keep.tile([P, (b - a) * D], BF16, name="xraw%d_%d" % (g, a))
-            rows = x[512 * g : 512 * (g + 1), :].rearrange("(m t) k -> m (t k)", t=4)
-            nc.sync.dma_start(out=xt[:], in_=rows[:, a * D : b * D])
+            rows = x.rearrange("(b j r t) k -> j b r (t k)", j=G, r=8, t=4)[g]
+            nc.sync.dma_start(out=xt[:], in_=rows[:, :, a * D : b * D])
             for t in range(a, b):
                 xraw[g, t] = xt[:, (t - a) * D : (t - a + 1) * D]
                 for end in range(t + 1, b + 1):
@@ -85,38 +83,33 @@ def tile_lhuc_senone_gradient_s13_kernel(tc, x, w, lhuc, err_words, err_scales, 
                     in_=w[512 * q : 512 * (q + 1), WC * c : WC * (c + 1)].rearrange("(p j) n -> p j n", j=4),
                 )
 
-        def load_lhuc_spread(c):
-            rows = lhuc.rearrange("(g s) n -> s g n", s=2)
-            for s in range(2):
-                nc.sync.dma_start(
-                    out=lraw[c - 2][64 * s : 64 * (s + 1), :, :],
-                    in_=rows[s, :, WC * c : WC * (c + 1)].partition_broadcast(64),
-                )
-
         def load_esca(a):
-            rows = err_scales.rearrange("g (k r) n -> r k g n", r=4)
+            rows = err_scales.rearrange("k (r j) n -> r k j n", j=G)
             for r in range(4):
                 nc.sync.dma_start(out=esca[a][r:P:32, :, :].bitcast(I32), in_=rows[r, :, 2 * a : 2 * a + 2, :].bitcast(I32))
 
         def load_ewor(g):
-            nc.sync.dma_start(out=ewor[g][:].bitcast(I32), in_=err_words[g].bitcast(I32))
+            nc.sync.dma_start(out=ewor[g][:].bitcast(I32), in_=err_words.rearrange("k (b j r) n -> j (k b) r n", j=G, r=8)[g].bitcast(I32))
 
         xgrp = {}
         xord = {}
 
-        def xsort(g, lo, hi):
-            xo = work.tile([P, (hi - lo) * 512], F32, name="xo", tag="xo", bufs=3)
-            nc.vector.tensor_copy(
-                out=xo[:].rearrange("p (a u m) -> p a m u", u=2, m=P),
-                in_=xrun[g, lo, hi].bitcast(F32).rearrange("p (a m u) -> p a m u", u=2, m=P),
+        def xsort(g, lo, hi, eng):
+            xo = work.tile([P, (hi - lo) * 512], F32, name="xo", tag="xo", bufs=4)
+            copy_on(
+                eng,
+                xo[:].rearrange("p (a u m) -> p a m u", u=2, m=P),
+                xrun[g, lo, hi].bitcast(F32).rearrange("p (a m u) -> p a m u", u=2, m=P),
             )
             for t in range(lo, hi):
                 xord[g, t] = xo[:, 512 * (t - lo) : 512 * (t - lo + 1)]
 
-        def trans(g, t):
-            b = take(("x", g, t), [P, 512])
+        def trans(g, t, passes=range(Q)):
+            if passes[0] == 0:
+                xbank[g, t] = take(("x", g, t), [P, 512])
+            b = xbank[g, t]
             words = xraw[g, t].bitcast(F32)
-            for q in range(Q):
+            for q in passes:
                 for u in range(2):
                     j = 2 * q + u
                     if (g, t) in xord:
@@ -124,36 +117,39 @@ def tile_lhuc_senone_gradient_s13_kernel(tc, x, w, lhuc, err_words, err_scales, 
                     else:
                         cols = words[:, 256 * q + u : 256 * (q + 1) : 2]
                     nc.tensor.transpose(b[:, P * j : P * (j + 1)], cols, ident[:])
-            xbank[g, t] = b
 
         xbank = {}
 
-        def xevict(g, t, eng):
-            if t % 2 == 0:
+        def xevict(g, t, eng, passes=range(Q)):
+            if (g, t // 2) not in xgrp:
                 xgrp[g, t // 2] = work.tile([P, 2 * D], BF16, name="xg", tag="xg", bufs=3, align_bytes=64)
+            lo, hi = passes[0], passes[-1] + 1
+            dst = xgrp[g, t // 2][:, D * (t % 2) + 512 * lo : D * (t % 2) + 512 * hi]
             copy_on(
                 eng,
-                xgrp[g, t // 2][:, D * (t % 2) : D * (t % 2 + 1)].bitcast(F32).rearrange("p (q m u) -> p q m u", q=Q, u=2),
-                xbank[g, t][:].rearrange("p (q u m) -> p q m u", q=Q, u=2),
+                dst.bitcast(F32).rearrange("p (q m u) -> p q m u", m=P, u=2),
+                xbank[g, t][:, 256 * lo : 256 * hi].rearrange("p (q u m) -> p q m u", m=P, u=2),
             )
-            give(("x", g, t))
+            if hi == Q:
+                give(("x", g, t))
 
         def xquant(g, lo, hi):
+            first = 2 * Q * (lo // (2 * Q))
             nc.vector.quantize_mx(
-                out=xcod[g][:, Q * P * lo : Q * P * hi].bitcast(FP8X4),
-                scales=xsca[g][:, Q * P * lo : Q * P * hi],
-                in_=xgrp[g, lo // 2][:, D * (lo % 2) : D * (lo % 2 + hi - lo)],
+                out=xcod[g][:, P * lo : P * hi].bitcast(FP8X4),
+                scales=xsca[g][:, P * lo : P * hi],
+                in_=xgrp[g, lo // (2 * Q)][:, 512 * (lo - first) : 512 * (hi - first)],
             )
 
         wgrp = {}
 
-        def winter(c, q, eng):
+        def winter(c, q, eng, lo=0, hi=WC):
             if c not in wgrp:
                 wgrp[c] = work.tile([P, Q * WC * 4], BF16, name="wg", tag="wg", bufs=2, align_bytes=64)
             copy_on(
                 eng,
-                wgrp[c][:, 4 * WC * q : 4 * WC * (q + 1)].rearrange("p (c i j) -> p c j i", i=4, j=4),
-                wraw[c][q][:].rearrange("p j (c i) -> p c j i", i=4),
+                wgrp[c][:, 4 * (WC * q + lo) : 4 * (WC * q + hi)].rearrange("p (c i j) -> p c j i", i=4, j=4),
+                wraw[c][q][:, :, lo:hi].rearrange("p j (c i) -> p c j i", i=4),
             )
 
         def wquant(c, lo, hi):
@@ -166,28 +162,26 @@ def tile_lhuc_senone_gradient_s13_kernel(tc, x, w, lhuc, err_words, err_scales, 
         abank = {}
 
         def lhuc_turn():
-            b = take("turn", [P, P])
-            nc.tensor.transpose(b[:], lrow[:].bitcast(F32), ident[:])
-            nc.vector.tensor_copy(out=lcol[:].rearrange("p s c -> p (s c)"), in_=b[:, 0 : SPK * NC])
-            give("turn")
+            abank["turn"] = take("turn", [P, P])
+            nc.tensor.transpose(abank["turn"][:], lrow[:].bitcast(F32), ident[:])
 
-        def lhuc_repeat(c):
-            nc.vector.tensor_copy(out=lrep[c][:], in_=lcol[:, :, c : c + 1].to_broadcast([P, SPK, 64]))
+        def lhuc_repeat(lo, hi):
+            cols = abank["turn"][:, 0 : SPK * NC].rearrange("p (s c) -> p c s", c=NC)[:, lo:hi, :]
+            nc.vector.tensor_copy(
+                out=lrep[:, lo:hi, :].rearrange("p c (s r) -> p c s r", s=SPK),
+                in_=cols.unsqueeze(3).to_broadcast([P, hi - lo, SPK, P // SPK]),
+            )
+            if hi == NC:
+                give("turn")
 
-        def lhuc_spread(c):
-            b = take(("amp", c), [P, G, P])
-            for g in range(G):
-                nc.tensor.transpose(b[:, g, :], lrep[c][:, 2 * g : 2 * g + 2, :].rearrange("p s r -> p (s r)"), ident[:])
-            abank[c] = b
+        def lhuc_spread(lo, hi):
+            abank[lo] = take(("amp", lo), [P, (hi - lo) * P])
+            for c in range(lo, hi):
+                nc.tensor.transpose(abank[lo][:, P * (c - lo) : P * (c - lo + 1)], lrep[:, c, :], ident[:])
 
-        def sigm(c, lo, hi):
-            if c < 2:
-                src = abank[c][:, lo:hi, :].bitcast(BF16)
-            else:
-                src = lraw[c - 2][:, lo:hi, :]
-            nc.scalar.activation(out=amp[c][:, lo:hi, :], in_=src, func=ACT.Sigmoid)
-            if c < 2 and hi == G:
-                give(("amp", c))
+        def sigm(lo, hi):
+            nc.scalar.activation(out=amp[:, WC * lo : WC * hi], in_=abank[lo][:].bitcast(BF16), func=ACT.Sigmoid)
+            give(("amp", lo))
 
         halves = {}
         zb = {}
@@ -198,8 +192,8 @@ def tile_lhuc_senone_gradient_s13_kernel(tc, x, w, lhuc, err_words, err_scales, 
                 if u == 0:
                     halves[g, c] = work.tile([P, 2, WC, 2], BF16, name="half", tag="half", bufs=3, align_bytes=64)
                 zb[g, c, u] = take(("z", g, c, u), [P, 2, WC])
-            for q in passes:
-                for e in range(2):
+            for e in range(2):
+                for q in passes:
                     t = 2 * u + e
                     nc.tensor.matmul_mx(
                         out=zb[g, c, u][:, e, :],
@@ -216,7 +210,7 @@ def tile_lhuc_senone_gradient_s13_kernel(tc, x, w, lhuc, err_words, err_scales, 
                 out=halves[g, c][:, u, :, :],
                 in0=zb[g, c, u][:].rearrange("p e n -> p n e"),
                 scalar=0.0,
-                in1=amp[c][:, g, :].unsqueeze(2).to_broadcast([P, WC, 2]),
+                in1=amp[:, WC * c : WC * (c + 1)].unsqueeze(2).to_broadcast([P, WC, 2]),
                 op0=ALU.max,
                 op1=ALU.mult,
             )
@@ -272,11 +266,13 @@ def tile_lhuc_senone_gradient_s13_kernel(tc, x, w, lhuc, err_words, err_scales, 
             for plane in esca:
                 nc.vector.memset(plane[:].rearrange("p g n -> p (g n)").bitcast(I32), 0)
             load_x(0, 0, 1)
+            load_w(0, [0])
             load_x(0, 1, 2)
-            load_w(0)
+            load_w(0, [1])
             load_x(0, 2, 3)
             load_x(0, 3, 4)
-            load_x(1, 0, 2)
+            load_x(1, 0, 1)
+            load_x(1, 1, 2)
             load_x(1, 2, 4)
             load_x(2, 0, 2)
             load_x(2, 2, 4)
@@ -291,8 +287,6 @@ def tile_lhuc_senone_gradient_s13_kernel(tc, x, w, lhuc, err_words, err_scales, 
             load_ewor(3)
             load_w(2)
             load_w(3)
-            load_lhuc_spread(2)
-            load_lhuc_spread(3)
 
             def stage(k, c):
                 g, u = divmod(k, 2)
@@ -311,135 +305,154 @@ def tile_lhuc_senone_gradient_s13_kernel(tc, x, w, lhuc, err_words, err_scales, 
                 for n in banks:
                     s2(h, 512 * n, 512 * (n + 1), [g])
 
-            lhuc_turn()
-            lhuc_repeat(0)
-            trans(0, 0)
-            lhuc_repeat(1)
-            xevict(0, 0, "v")
-            trans(0, 1)
-            lhuc_spread(0)
-            sigm(0, 0, 1)
-            xevict(0, 1, "s")
-            sigm(0, 1, G)
-            lhuc_spread(1)
-            winter(0, 0, "v")
-            xquant(0, 0, 1)
-            winter(0, 1, "v")
-            trans(0, 2)
-            xevict(0, 2, "s")
-            wquant(0, 0, 1)
-            wquant(0, 1, 2)
-            xquant(0, 1, 2)
-            trans(0, 3)
-            xevict(0, 3, "s")
-            sigm(1, 0, 2)
-
             def turn(g, lo, hi):
                 for t in range(lo, hi):
                     trans(g, t)
                     xevict(g, t, "s")
 
+            def half(g, c, u):
+                s1(g, c, u)
+                hevict(g, c, u)
+
+            lhuc_turn()
+            lhuc_repeat(0, 1)
+            lhuc_repeat(1, NC)
+            trans(0, 0, [0])
+            lhuc_spread(0, 1)
+            trans(0, 0, [1])
+            sigm(0, 1)
+            xevict(0, 0, "s")
+            trans(0, 1)
+            xevict(0, 1, "s")
+            lhuc_spread(1, NC)
+            winter(0, 0, "v")
+            wquant(0, 0, 1)
+            winter(0, 1, "v")
+            xquant(0, 0, 2)
+            wquant(0, 1, 2)
+            xquant(0, 2, 4)
+            turn(0, 2, 3)
             s1(0, 0, 0)
-            xquant(0, 2, 3)
-            xsort(1, 1, 2)
-            xquant(0, 3, 4)
-            turn(1, 0, 2)
+
+            sigm(1, NC)
+            xsort(1, 0, 1, "v")
+            xsort(1, 1, 2, "v")
+            xquant(0, 4, 6)
+            trans(0, 3)
+            xevict(0, 3, "s", [0])
+            xevict(0, 3, "s", [1])
             hevict(0, 0, 0)
-            xsort(1, 2, 3)
+            xsort(1, 3, 4, "v")
+            xquant(0, 6, 7)
+            xquant(0, 7, 8)
+            turn(1, 0, 3)
             s1(0, 0, 1)
-            turn(1, 2, 4)
-            xquant(1, 0, 1)
-            xquant(1, 1, 2)
-            s1(1, 0, 0)
-            xsort(2, 0, 1)
-            hevict(0, 0, 1)
-            xsort(2, 3, 4)
-            xquant(1, 2, 4)
+            xsort(2, 0, 2, "v")
+            xquant(1, 0, 4)
+            turn(1, 3, 4)
             turn(2, 0, 2)
-            hjoin(0, 0, "s")
+            xsort(2, 2, 4, "v")
+            s1(1, 0, 0)
+            xquant(1, 4, 8)
+            xquant(2, 0, 2)
+            hevict(0, 0, 1)
             turn(2, 2, 4)
-            hevict(1, 0, 0)
-            s1(1, 0, 1)
-            xquant(2, 0, 1)
-            xquant(2, 1, 2)
-            s1(2, 0, 0)
-            xsort(3, 0, 2)
-            xsort(3, 2, 3)
-            sigm(1, 2, G)
-            hevict(1, 0, 1)
+            hjoin(0, 0, "s")
             xquant(2, 2, 4)
+            s1(1, 0, 1)
+            s1(2, 0, 0)
+            xsort(3, 0, 2, "v")
+            xsort(3, 2, 3, "v")
+            xquant(2, 4, 8)
             hquant(0, 0)
-            turn(3, 0, 2)
-            hjoin(1, 0, "s")
-            turn(3, 2, 4)
-            hevict(2, 0, 0)
+            for t in range(4):
+                trans(3, t)
             s1(2, 0, 1)
-            s2row(0, 0, [0, 1])
-            xquant(3, 0, 1)
-            xquant(3, 1, 2)
-            hquant(1, 0)
+            xevict(3, 0, "s")
+            hevict(1, 0, 0)
+            xevict(3, 1, "s")
+            hevict(1, 0, 1)
+            xevict(3, 2, "s")
+            xevict(3, 3, "s")
+            hjoin(1, 0, "s")
+            xquant(3, 0, 4)
+            s2row(0, 0, [0, 1, 2])
+            s2row(1, 0, [0, 1])
             s1(3, 0, 0)
-            hevict(2, 0, 1)
-            xquant(3, 2, 4)
-            hjoin(2, 0, "s")
+            hevict(2, 0, 0)
+            xquant(3, 4, 8)
+            hquant(1, 0)
+            s1(3, 0, 1)
             winter(1, 0, "s")
+            winter(1, 1, "s", 0, 128)
+            hevict(2, 0, 1)
+            hjoin(2, 0, "s")
+            winter(1, 1, "s", 128, 256)
             hevict(3, 0, 0)
-            s2row(0, 1, [0, 1])
-            s2row(0, 0, [2])
-            s2row(0, 1, [2])
-            s2row(1, 0, [0])
-            s2row(1, 1, [0])
-            hquant(G - 2, 0)
-            winter(1, 1, "v")
-            s1(G - 1, 0, 1)
-            hevict(G - 1, 0, 1)
-            hjoin(G - 1, 0, "s")
-            wquant(1, 0, 2)
-            winter(2, 0, "s")
-            s2row(1, 0, [1])
-            s2row(1, 1, [1])
+            hevict(3, 0, 1)
+            hjoin(3, 0, "s")
+            s2row(0, 1, [0, 1, 2])
+            s2row(1, 1, [0, 1])
+            s2row(1, 0, [2])
+            s2row(1, 1, [2])
+            hquant(2, 0)
+            wquant(1, 0, 1)
+            wquant(1, 1, 2)
+            hquant(3, 0)
             s2row(0, 2, [0, 1, 2])
-            s2row(1, 2, [0, 1])
             s1(0, 1, 0)
-            hquant(G - 1, 0)
             hevict(0, 1, 0)
-            stage(1, 1)
-            for n in range(NS):
-                s2row(0, 3, [n])
-                finish(0, n)
+
+            s1(0, 1, 1)
+            hevict(0, 1, 1)
+            hjoin(0, 1, "s")
+            s2row(1, 2, [0, 1])
+            half(1, 1, 0)
+            winter(2, 0, "v")
+            s2row(0, 3, [0])
+            finish(0, 0)
+            s2row(0, 3, [1])
+            finish(0, 1)
+            half(1, 1, 1)
+            hquant(0, 1)
+            hjoin(1, 1, "s")
+            s2row(0, 3, [2])
+            finish(0, 2)
+            s2row(1, 3, [0])
+            finish(1, 0)
+            half(2, 1, 0)
             winter(2, 1, "v")
-            stage(2, 1)
-            stage(3, 1)
-            for n in range(2):
-                s2row(1, 3, [n])
-                finish(1, n)
-            stage(4, 1)
-            wquant(2, 0, 2)
-            stage(5, 1)
-            s2(1, 1024, 1536, range(G))
+            s2row(1, 3, [1])
+            finish(1, 1)
+            half(2, 1, 1)
+            hquant(1, 1)
+            hjoin(2, 1, "s")
+            s2row(1, 2, [2])
+            s2row(1, 3, [2])
             finish(1, 2)
-            sigm(2, 0, 2)
-            stage(6, 1)
-            winter(3, 0, "v")
-            s2row(2, 0, [0, 1, 2])
+            half(3, 1, 0)
+            wquant(2, 0, 2)
+            s2row(2, 0, [0, 1])
+            half(3, 1, 1)
             hquant(2, 1)
-            stage(7, 1)
-            sigm(2, 2, G)
-            s2row(2, 1, [0, 1, 2])
+            hjoin(3, 1, "s")
+            winter(3, 0, "s")
+            s2row(2, 0, [2])
             s2row(3, 0, [0])
+            s2row(2, 1, [0, 1, 2])
             s2row(3, 1, [0])
-            hquant(G - 1, 1)
-            winter(3, 1, "v")
+            hquant(3, 1)
+            half(0, 2, 0)
             s2row(2, 2, [0, 1, 2])
             s2row(3, 2, [0])
-            wquant(3, 0, 2)
+            winter(3, 1, "s")
             share = [1, 2, 2, 2, 1, 0]
             for c in range(1, NC):
-                k = 0
+                k = 1 if c == 1 else 0
                 for i in range(2 * NS):
                     h, n = 2 * c + i // NS, i % NS
                     if c + 1 < NC:
-                        for j in range(share[i]):
+                        for j in range(share[i] - (c == 1 and i == 1)):
                             stage(k, c + 1)
                             k += 1
                     if i == 5 and c + 1 < NC:
@@ -448,9 +461,8 @@ def tile_lhuc_senone_gradient_s13_kernel(tc, x, w, lhuc, err_words, err_scales, 
                         break
                     s2(h, 512 * n, 512 * (n + 1), [G - 1] if c == 1 and i < 4 else range(G))
                     finish(h, n)
-                    if c + 2 < NC:
-                        if i in (2, 4):
-                            sigm(c + 2, i - 2, i)
+                    if c == 1 and i == 3:
+                        wquant(3, 0, 2)
             cuts = [0, 512, 768, 1024, 1280, 1408, S]
             for i in range(len(cuts) - 1):
                 s2(NH - 1, cuts[i], cuts[i + 1], range(G))

@@ -35,8 +35,10 @@ def tile_lhuc_senone_gradient_s13_kernel(tc, x, w, lhuc, err_words, err_scales, 
 
         ident = keep.tile([P, P], F32, name="ident")
         lrow = keep.tile([P, WC], BF16, name="lrow", align_bytes=64)
-        lrep = keep.tile([P, NC, P], F32, name="lrep", align_bytes=64)
-        amp = keep.tile([P, H], F32, name="amp")
+        lrep = [keep.tile([P, SPK, 64], F32, name="lrep%d" % c, align_bytes=64) for c in range(2)]
+        lcol = keep.tile([P, SPK, NC], F32, name="lcol")
+        lraw = [keep.tile([P, G, WC], BF16, name="lraw%d" % c) for c in range(1, NC)]
+        amp = [keep.tile([P, G, WC], F32, name="amp%d" % c) for c in range(NC)]
         xcod = [keep.tile([P, 4 * Q * P], U32, name="xcod%d" % g, align_bytes=64) for g in range(G)]
         xsca = [keep.tile([P, 4 * Q * P], U8, name="xsca%d" % g, align_bytes=64) for g in range(G)]
         wraw = [[keep.tile([P, 4, WC], BF16, name="wraw%d_%d" % (c, q)) for q in range(Q)] for c in range(NC)]
@@ -69,8 +71,8 @@ def tile_lhuc_senone_gradient_s13_kernel(tc, x, w, lhuc, err_words, err_scales, 
 
         def load_x(g, a, b):
             xt = keep.tile([P, (b - a) * D], BF16, name="xraw%d_%d" % (g, a))
-            rows = x.rearrange("(b j r t) k -> j b r (t k)", j=G, r=8, t=4)[g]
-            nc.sync.dma_start(out=xt[:], in_=rows[:, :, a * D : b * D])
+            rows = x[512 * g : 512 * (g + 1), :].rearrange("(m t) k -> m (t k)", t=4)
+            nc.sync.dma_start(out=xt[:], in_=rows[:, a * D : b * D])
             for t in range(a, b):
                 xraw[g, t] = xt[:, (t - a) * D : (t - a + 1) * D]
                 for end in range(t + 1, b + 1):
@@ -83,13 +85,21 @@ def tile_lhuc_senone_gradient_s13_kernel(tc, x, w, lhuc, err_words, err_scales, 
                     in_=w[512 * q : 512 * (q + 1), WC * c : WC * (c + 1)].rearrange("(p j) n -> p j n", j=4),
                 )
 
+        def load_lhuc_spread(c):
+            rows = lhuc.rearrange("(g s) n -> s g n", s=2)
+            for s in range(2):
+                nc.sync.dma_start(
+                    out=lraw[c - 1][64 * s : 64 * (s + 1), :, :],
+                    in_=rows[s, :, WC * c : WC * (c + 1)].partition_broadcast(64),
+                )
+
         def load_esca(a):
-            rows = err_scales.rearrange("k (r j) n -> r k j n", j=G)
+            rows = err_scales.rearrange("g (k r) n -> r k g n", r=4)
             for r in range(4):
                 nc.sync.dma_start(out=esca[a][r:P:32, :, :].bitcast(I32), in_=rows[r, :, 2 * a : 2 * a + 2, :].bitcast(I32))
 
         def load_ewor(g):
-            nc.sync.dma_start(out=ewor[g][:].bitcast(I32), in_=err_words.rearrange("k (b j r) n -> j (k b) r n", j=G, r=8)[g].bitcast(I32))
+            nc.sync.dma_start(out=ewor[g][:].bitcast(I32), in_=err_words[g].bitcast(I32))
 
         xgrp = {}
         xord = {}
@@ -165,23 +175,32 @@ def tile_lhuc_senone_gradient_s13_kernel(tc, x, w, lhuc, err_words, err_scales, 
             abank["turn"] = take("turn", [P, P])
             nc.tensor.transpose(abank["turn"][:], lrow[:].bitcast(F32), ident[:])
 
-        def lhuc_repeat(lo, hi):
-            cols = abank["turn"][:, 0 : SPK * NC].rearrange("p (s c) -> p c s", c=NC)[:, lo:hi, :]
+        def lhuc_keep():
+            nc.vector.tensor_copy(out=lcol[:].rearrange("p s c -> p (s c)"), in_=abank["turn"][:, 0 : SPK * NC])
+
+        def lhuc_repeat(c, lo, hi, cols):
             nc.vector.tensor_copy(
-                out=lrep[:, lo:hi, :].rearrange("p c (s r) -> p c s r", s=SPK),
-                in_=cols.unsqueeze(3).to_broadcast([P, hi - lo, SPK, P // SPK]),
+                out=lrep[c][:, 2 * lo : 2 * hi, :],
+                in_=cols[:, 2 * lo : 2 * hi, c : c + 1].to_broadcast([P, 2 * (hi - lo), 64]),
             )
-            if hi == NC:
-                give("turn")
 
-        def lhuc_spread(lo, hi):
-            abank[lo] = take(("amp", lo), [P, (hi - lo) * P])
-            for c in range(lo, hi):
-                nc.tensor.transpose(abank[lo][:, P * (c - lo) : P * (c - lo + 1)], lrep[:, c, :], ident[:])
+        def lhuc_spread(c, lo, hi):
+            abank[c, lo] = take(("amp", c, lo), [P, (hi - lo) * P])
+            for g in range(lo, hi):
+                cols = lrep[c][:, 2 * g : 2 * g + 2, :].rearrange("p s r -> p (s r)")
+                nc.tensor.transpose(abank[c, lo][:, P * (g - lo) : P * (g - lo + 1)], cols, ident[:])
 
-        def sigm(lo, hi):
-            nc.scalar.activation(out=amp[:, WC * lo : WC * hi], in_=abank[lo][:].bitcast(BF16), func=ACT.Sigmoid)
-            give(("amp", lo))
+        def lhuc_park(c):
+            nc.scalar.copy(out=lraw[c - 1][:].rearrange("p g n -> p (g n)").bitcast(F32), in_=abank[c, 0][:])
+            give(("amp", c, 0))
+
+        def sigm(c, lo, hi):
+            dst = amp[c][:, lo:hi, :].rearrange("p g n -> p (g n)")
+            if c == 0:
+                nc.scalar.activation(out=dst, in_=abank[c, lo][:].bitcast(BF16), func=ACT.Sigmoid)
+                give(("amp", c, lo))
+            else:
+                nc.scalar.activation(out=dst, in_=lraw[c - 1][:, lo:hi, :].rearrange("p g n -> p (g n)"), func=ACT.Sigmoid)
 
         halves = {}
         zb = {}
@@ -210,7 +229,7 @@ def tile_lhuc_senone_gradient_s13_kernel(tc, x, w, lhuc, err_words, err_scales, 
                 out=halves[g, c][:, u, :, :],
                 in0=zb[g, c, u][:].rearrange("p e n -> p n e"),
                 scalar=0.0,
-                in1=amp[:, WC * c : WC * (c + 1)].unsqueeze(2).to_broadcast([P, WC, 2]),
+                in1=amp[c][:, g, :].unsqueeze(2).to_broadcast([P, WC, 2]),
                 op0=ALU.max,
                 op1=ALU.mult,
             )
@@ -276,8 +295,8 @@ def tile_lhuc_senone_gradient_s13_kernel(tc, x, w, lhuc, err_words, err_scales, 
             load_x(1, 2, 4)
             load_x(2, 0, 2)
             load_x(2, 2, 4)
-            load_x(3, 0, 2)
-            load_x(3, 2, 4)
+            load_x(3, 0, 3)
+            load_x(3, 3, 4)
             load_esca(0)
             load_ewor(0)
             load_ewor(1)
@@ -287,6 +306,8 @@ def tile_lhuc_senone_gradient_s13_kernel(tc, x, w, lhuc, err_words, err_scales, 
             load_ewor(3)
             load_w(2)
             load_w(3)
+            load_lhuc_spread(2)
+            load_lhuc_spread(3)
 
             def stage(k, c):
                 g, u = divmod(k, 2)
@@ -315,17 +336,22 @@ def tile_lhuc_senone_gradient_s13_kernel(tc, x, w, lhuc, err_words, err_scales, 
                 hevict(g, c, u)
 
             lhuc_turn()
-            lhuc_repeat(0, 1)
-            lhuc_repeat(1, NC)
+            lhuc_keep()
+            lhuc_repeat(0, 0, 1, abank["turn"][:, 0 : SPK * NC].rearrange("p (s c) -> p s c", c=NC))
+            give("turn")
+            lhuc_repeat(0, 1, G, lcol)
             trans(0, 0, [0])
-            lhuc_spread(0, 1)
+            lhuc_spread(0, 0, 1)
             trans(0, 0, [1])
-            sigm(0, 1)
+            sigm(0, 0, 1)
             xevict(0, 0, "s")
+            lhuc_spread(0, 1, G)
             trans(0, 1)
             xevict(0, 1, "s")
-            lhuc_spread(1, NC)
             winter(0, 0, "v")
+            lhuc_repeat(1, 0, G, lcol)
+            lhuc_spread(1, 0, G)
+            lhuc_park(1)
             wquant(0, 0, 1)
             winter(0, 1, "v")
             xquant(0, 0, 2)
@@ -334,7 +360,7 @@ def tile_lhuc_senone_gradient_s13_kernel(tc, x, w, lhuc, err_words, err_scales, 
             turn(0, 2, 3)
             s1(0, 0, 0)
 
-            sigm(1, NC)
+            sigm(0, 1, G)
             xsort(1, 0, 1, "v")
             xsort(1, 1, 2, "v")
             xquant(0, 4, 6)
@@ -361,8 +387,8 @@ def tile_lhuc_senone_gradient_s13_kernel(tc, x, w, lhuc, err_words, err_scales, 
             xquant(2, 2, 4)
             s1(1, 0, 1)
             s1(2, 0, 0)
-            xsort(3, 0, 2, "v")
-            xsort(3, 2, 3, "v")
+            xsort(3, 0, 1, "v")
+            xsort(3, 1, 3, "v")
             xquant(2, 4, 8)
             hquant(0, 0)
             for t in range(4):
@@ -395,6 +421,8 @@ def tile_lhuc_senone_gradient_s13_kernel(tc, x, w, lhuc, err_words, err_scales, 
             s2row(1, 1, [0, 1])
             s2row(1, 0, [2])
             s2row(1, 1, [2])
+            sigm(1, 0, 1)
+            sigm(1, 1, G)
             hquant(2, 0)
             wquant(1, 0, 1)
             wquant(1, 1, 2)
@@ -436,6 +464,8 @@ def tile_lhuc_senone_gradient_s13_kernel(tc, x, w, lhuc, err_words, err_scales, 
             half(3, 1, 1)
             hquant(2, 1)
             hjoin(3, 1, "s")
+            sigm(2, 0, 2)
+            sigm(2, 2, G)
             winter(3, 0, "s")
             s2row(2, 0, [2])
             s2row(3, 0, [0])
@@ -463,6 +493,8 @@ def tile_lhuc_senone_gradient_s13_kernel(tc, x, w, lhuc, err_words, err_scales, 
                     finish(h, n)
                     if c == 1 and i == 3:
                         wquant(3, 0, 2)
+                    if c == 1 and i in (3, 4):
+                        sigm(3, 2 * (i - 3), 2 * (i - 2))
             cuts = [0, 512, 768, 1024, 1280, 1408, S]
             for i in range(len(cuts) - 1):
                 s2(NH - 1, cuts[i], cuts[i + 1], range(G))

@@ -299,14 +299,14 @@ def tile_lhuc_senone_gradient_s13_kernel(tc, x, w, lhuc, err_words, err_scales, 
             load_x(3, 3, 4)
             load_esca(0)
             load_ewor(0)
-            load_ewor(1)
             load_w(1)
+            load_ewor(1)
             load_esca(1)
             load_ewor(2)
             load_ewor(3)
             load_w(2)
-            load_w(3)
             load_lhuc_spread(2)
+            load_w(3)
             load_lhuc_spread(3)
 
             def stage(k, c):
@@ -373,7 +373,7 @@ def tile_lhuc_senone_gradient_s13_kernel(tc, x, w, lhuc, err_words, err_scales, 
             xquant(0, 7, 8)
             turn(1, 0, 3)
             s1(0, 0, 1)
-            xsort(2, 0, 2, "v")
+            xsort(2, 0, 1, "v")
             xquant(1, 0, 4)
             turn(1, 3, 4)
             turn(2, 0, 2)
@@ -388,7 +388,7 @@ def tile_lhuc_senone_gradient_s13_kernel(tc, x, w, lhuc, err_words, err_scales, 
             s1(1, 0, 1)
             s1(2, 0, 0)
             xsort(3, 0, 1, "v")
-            xsort(3, 1, 3, "v")
+            xsort(3, 1, 2, "v")
             xquant(2, 4, 8)
             hquant(0, 0)
             for t in range(4):
@@ -410,38 +410,37 @@ def tile_lhuc_senone_gradient_s13_kernel(tc, x, w, lhuc, err_words, err_scales, 
             hquant(1, 0)
             s1(3, 0, 1)
             winter(1, 0, "s")
-            winter(1, 1, "s", 0, 128)
+            winter(1, 1, "s")
             hevict(2, 0, 1)
             hjoin(2, 0, "s")
-            winter(1, 1, "s", 128, 256)
             hevict(3, 0, 0)
+            wquant(1, 0, 1)
+            wquant(1, 1, 2)
             hevict(3, 0, 1)
+            sigm(1, 0, 1)
             hjoin(3, 0, "s")
             s2row(0, 1, [0, 1, 2])
             s2row(1, 1, [0, 1])
             s2row(1, 0, [2])
             s2row(1, 1, [2])
-            sigm(1, 0, 1)
             sigm(1, 1, G)
             hquant(2, 0)
-            wquant(1, 0, 1)
-            wquant(1, 1, 2)
-            hquant(3, 0)
-            s2row(0, 2, [0, 1, 2])
             s1(0, 1, 0)
             hevict(0, 1, 0)
+            hquant(3, 0)
 
             s1(0, 1, 1)
             hevict(0, 1, 1)
             hjoin(0, 1, "s")
-            s2row(1, 2, [0, 1])
+            s2row(0, 2, [0, 1, 2])
             half(1, 1, 0)
             winter(2, 0, "v")
+            s2row(1, 2, [0, 1])
+            half(1, 1, 1)
             s2row(0, 3, [0])
             finish(0, 0)
             s2row(0, 3, [1])
             finish(0, 1)
-            half(1, 1, 1)
             hquant(0, 1)
             hjoin(1, 1, "s")
             s2row(0, 3, [2])
@@ -458,43 +457,78 @@ def tile_lhuc_senone_gradient_s13_kernel(tc, x, w, lhuc, err_words, err_scales, 
             s2row(1, 2, [2])
             s2row(1, 3, [2])
             finish(1, 2)
-            half(3, 1, 0)
+            sigm(2, 0, 2)
             wquant(2, 0, 2)
+            half(3, 1, 0)
             s2row(2, 0, [0, 1])
             half(3, 1, 1)
             hquant(2, 1)
             hjoin(3, 1, "s")
-            sigm(2, 0, 2)
-            sigm(2, 2, G)
-            winter(3, 0, "s")
             s2row(2, 0, [2])
             s2row(3, 0, [0])
-            s2row(2, 1, [0, 1, 2])
-            s2row(3, 1, [0])
-            hquant(3, 1)
+            s2row(2, 1, [0])
+            sigm(2, 2, G)
             half(0, 2, 0)
-            s2row(2, 2, [0, 1, 2])
-            s2row(3, 2, [0])
+            hquant(3, 1)
+            s2row(2, 1, [1])
+            half(0, 2, 1)
+            hjoin(0, 2, "s")
             winter(3, 1, "s")
-            share = [1, 2, 2, 2, 1, 0]
-            for c in range(1, NC):
-                k = 1 if c == 1 else 0
-                for i in range(2 * NS):
-                    h, n = 2 * c + i // NS, i % NS
-                    if c + 1 < NC:
-                        for j in range(share[i] - (c == 1 and i == 1)):
-                            stage(k, c + 1)
-                            k += 1
-                    if i == 5 and c + 1 < NC:
-                        hquant(G - 1, c + 1)
-                    if h == NH - 1:
-                        break
-                    s2(h, 512 * n, 512 * (n + 1), [G - 1] if c == 1 and i < 4 else range(G))
-                    finish(h, n)
-                    if c == 1 and i == 3:
-                        wquant(3, 0, 2)
-                    if c == 1 and i in (3, 4):
-                        sigm(3, 2 * (i - 3), 2 * (i - 2))
+            s2row(2, 1, [2])
+            s2row(3, 1, [0])
+            half(1, 2, 0)
+            winter(3, 0, "v")
+            hquant(0, 2)
+            s2row(2, 2, [0, 1])
+            half(1, 2, 1)
+            hjoin(1, 2, "s")
+            sigm(3, 0, 2)
+            s2row(2, 2, [2])
+            s2row(3, 2, [0])
+            half(2, 2, 0)
+            hquant(1, 2)
+            for n in range(2):
+                s2row(2, 3, [n])
+                finish(2, n)
+            half(2, 2, 1)
+            hjoin(2, 2, "s")
+            wquant(3, 0, 2)
+            s2row(2, 3, [2])
+            finish(2, 2)
+            s2row(3, 3, [0])
+            finish(3, 0)
+            half(3, 2, 0)
+            hquant(2, 2)
+            s2(3, 512, 1024, [0, 1])
+            half(3, 2, 1)
+            hjoin(3, 2, "v")
+            s2(3, 512, 1024, [2, 3])
+            finish(3, 1)
+            hquant(3, 2)
+            s2(3, 1024, S, range(G))
+            finish(3, 2)
+            sigm(3, 2, G)
+            for i in range(2 * NS):
+                h, n = 4 + i // NS, i % NS
+                if i < G:
+                    half(i, 3, 0)
+                    if i > 0:
+                        hquant(i - 1, 3)
+                    half(i, 3, 1)
+                    hjoin(i, 3, "s")
+                if i == G:
+                    hquant(G - 1, 3)
+                if i == 0:
+                    s2(h, 0, 512, range(G - 1))
+                    continue
+                if i == 1:
+                    s2(h, 0, 512, [G - 1])
+                    finish(h, 0)
+                s2(h, 512 * n, 512 * (n + 1), range(G))
+                finish(h, n)
+            for n in range(NS):
+                s2(NH - 2, 512 * n, 512 * (n + 1), range(G))
+                finish(NH - 2, n)
             cuts = [0, 512, 768, 1024, 1280, 1408, S]
             for i in range(len(cuts) - 1):
                 s2(NH - 1, cuts[i], cuts[i + 1], range(G))

@@ -34,20 +34,20 @@ def tile_lhuc_senone_gradient_s13_kernel(tc, x, w, lhuc, err_words, err_scales, 
         psum = ctx.enter_context(tc.psum_pool(name="psum", bufs=1))
 
         ident = keep.tile([P, P], F32, name="ident")
-        lrow = keep.tile([P, WC], BF16, name="lrow", align_bytes=64)
+        lrow = keep.tile([P, WC], BF16, name="lrow", align_bytes=256)
         lrep = [keep.tile([P, SPK, 64], F32, name="lrep%d" % c, align_bytes=64) for c in range(2)]
         lcol = keep.tile([P, SPK, NC], F32, name="lcol")
-        lraw = [keep.tile([P, G, WC], BF16, name="lraw%d" % c) for c in range(1, NC)]
+        lraw = [keep.tile([P, G, WC], BF16, name="lraw%d" % c, align_bytes=256) for c in range(1, NC)]
         amp = [keep.tile([P, G, WC], F32, name="amp%d" % c) for c in range(NC)]
         xcod = [keep.tile([P, 4 * Q * P], U32, name="xcod%d" % g, align_bytes=64) for g in range(G)]
         xsca = [keep.tile([P, 4 * Q * P], U8, name="xsca%d" % g, align_bytes=64) for g in range(G)]
-        wraw = [[keep.tile([P, 4, WC], BF16, name="wraw%d_%d" % (c, q)) for q in range(Q)] for c in range(NC)]
+        wraw = [[keep.tile([P, 4, WC], BF16, name="wraw%d_%d" % (c, q), align_bytes=256) for q in range(Q)] for c in range(NC)]
         wcod = [keep.tile([P, Q * WC], U32, name="wcod%d" % c, align_bytes=64) for c in range(NC)]
         wsca = [keep.tile([P, Q * WC], U8, name="wsca%d" % c, align_bytes=64) for c in range(NC)]
         hcod = [keep.tile([P, G, WC], U32, name="hcod%d" % c, align_bytes=64) for c in range(NC)]
         hsca = [keep.tile([P, G, WC], U8, name="hsca%d" % c, align_bytes=64) for c in range(NC)]
-        ewor = [keep.tile([P, 2 * S], U8, name="ewor%d" % g, align_bytes=64) for g in range(G)]
-        esca = [keep.tile([P, 2, S], U8, name="esca%d" % a, align_bytes=64) for a in range(G // 2)]
+        ewor = [keep.tile([P, 2 * S], U8, name="ewor%d" % g, align_bytes=256) for g in range(G)]
+        esca = [keep.tile([P, 2, S], U8, name="esca%d" % a, align_bytes=256) for a in range(G // 2)]
 
         free = list(range(8))
         held = {}
@@ -70,7 +70,7 @@ def tile_lhuc_senone_gradient_s13_kernel(tc, x, w, lhuc, err_words, err_scales, 
         xrun = {}
 
         def load_x(g, a, b):
-            xt = keep.tile([P, (b - a) * D], BF16, name="xraw%d_%d" % (g, a))
+            xt = keep.tile([P, (b - a) * D], BF16, name="xraw%d_%d" % (g, a), align_bytes=256)
             rows = x[512 * g : 512 * (g + 1), :].rearrange("(m t) k -> m (t k)", t=4)
             nc.sync.dma_start(out=xt[:], in_=rows[:, a * D : b * D])
             for t in range(a, b):
@@ -266,7 +266,7 @@ def tile_lhuc_senone_gradient_s13_kernel(tc, x, w, lhuc, err_words, err_scales, 
 
         def oevict(h, lo, hi, eng):
             if h not in og:
-                og[h] = work.tile([P, S], F32, name="og", tag="og", bufs=3)
+                og[h] = work.tile([P, S], F32, name="og", tag="og", bufs=3, align_bytes=256)
             dst = og[h][:, lo:hi]
             if eng == "s":
                 nc.scalar.activation(out=dst, in_=ob[h, lo][:], func=ACT.Copy, scale=2.0)

@@ -298,10 +298,10 @@ def tile_lhuc_senone_gradient_s13_kernel(tc, x, w, lhuc, err_words, err_scales, 
             load_x(3, 0, 3)
             load_x(3, 3, 4)
             load_esca(0)
+            load_esca(1)
             load_ewor(0)
             load_w(1)
             load_ewor(1)
-            load_esca(1)
             load_ewor(2)
             load_ewor(3)
             load_w(2)

from contextlib import ExitStack

from concourse.masks import make_identity
import concourse.mybir as mybir

F32 = mybir.dt.float32
BF16 = mybir.dt.bfloat16
I32 = mybir.dt.int32
U32 = mybir.dt.uint32
U8 = mybir.dt.uint8
FP8X4 = mybir.dt.float8_e4m3fn_x4
FP4X4 = mybir.dt.float4_e2m1fn_x4
ALU = mybir.AluOpType
ACT = mybir.ActivationFunctionType

T, D, H, S, SPK = 2048, 1024, 1024, 1536, 8
P = 128
G = T // 512
Q = D // 512
NH = H // P
NS = S // 512
WC = 256
NC = H // WC

FLOPS = 2 * T * D * H + 2 * T * H * S
BYTES = 2 * T * D + 2 * D * H + 2 * SPK * H + T * S // 2 + T * S // 32 + 4 * H * S


def tile_lhuc_senone_gradient_s13_kernel(tc, x, w, lhuc, err_words, err_scales, out):
    nc = tc.nc
    with ExitStack() as ctx:
        keep = ctx.enter_context(tc.tile_pool(name="keep", bufs=1))
        work = ctx.enter_context(tc.tile_pool(name="work", bufs=4))
        psum = ctx.enter_context(tc.psum_pool(name="psum", bufs=1))

        ident = keep.tile([P, P], F32, name="ident")
        lrow = keep.tile([P, WC], BF16, name="lrow", align_bytes=256)
        lrep = [keep.tile([P, SPK, 64], F32, name="lrep%d" % c, align_bytes=64) for c in range(2)]
        lcol = keep.tile([P, SPK, NC], F32, name="lcol")
        lraw = [keep.tile([P, G, WC], BF16, name="lraw%d" % c, align_bytes=256) for c in range(1, NC)]
        amp = [keep.tile([P, G, WC], F32, name="amp%d" % c) for c in range(NC)]
        xcod = [keep.tile([P, 4 * Q * P], U32, name="xcod%d" % g, align_bytes=64) for g in range(G)]
        xsca = [keep.tile([P, 4 * Q * P], U8, name="xsca%d" % g, align_bytes=64) for g in range(G)]
        wraw = [[keep.tile([P, 4, WC], BF16, name="wraw%d_%d" % (c, q), align_bytes=256) for q in range(Q)] for c in range(NC)]
        wcod = [keep.tile([P, Q * WC], U32, name="wcod%d" % c, align_bytes=64) for c in range(NC)]
        wsca = [keep.tile([P, Q * WC], U8, name="wsca%d" % c, align_bytes=64) for c in range(NC)]
        hcod = [keep.tile([P, G, WC], U32, name="hcod%d" % c, align_bytes=64) for c in range(NC)]
        hsca = [keep.tile([P, G, WC], U8, name="hsca%d" % c, align_bytes=64) for c in range(NC)]
        ewor = [keep.tile([P, 2 * S], U8, name="ewor%d" % g, align_bytes=256) for g in range(G)]
        esca = [keep.tile([P, 2, S], U8, name="esca%d" % a, align_bytes=256) for a in range(G // 2)]

        free = list(range(8))
        held = {}

        def take(user, shape):
            held[user] = free.pop(0)
            b = psum.tile(shape, F32, name="bank%d" % held[user], tag="bank%d" % held[user])
            return b

        def give(user):
            free.append(held.pop(user))

        def copy_on(eng, dst, src):
            if eng == "s":
                nc.scalar.copy(out=dst, in_=src)
            else:
                nc.vector.tensor_copy(out=dst, in_=src)

        xraw = {}
        xrun = {}

        def load_x(g, a, b):
            xt = keep.tile([P, (b - a) * D], BF16, name="xraw%d_%d" % (g, a), align_bytes=256)
            rows = x[512 * g : 512 * (g + 1), :].rearrange("(m t) k -> m (t k)", t=4)
            nc.sync.dma_start(out=xt[:], in_=rows[:, a * D : b * D])
            for t in range(a, b):
                xraw[g, t] = xt[:, (t - a) * D : (t - a + 1) * D]
                for end in range(t + 1, b + 1):
                    xrun[g, t, end] = xt[:, (t - a) * D : (end - a) * D]

        def load_w(c, passes=range(Q)):
            for q in passes:
                nc.sync.dma_start(
                    out=wraw[c][q][:],
                    in_=w[512 * q : 512 * (q + 1), WC * c : WC * (c + 1)].rearrange("(p j) n -> p j n", j=4),
                )

        def load_lhuc_spread(c):
            rows = lhuc.rearrange("(g s) n -> s g n", s=2)
            for s in range(2):
                nc.sync.dma_start(
                    out=lraw[c - 1][64 * s : 64 * (s + 1), :, :],
                    in_=rows[s, :, WC * c : WC * (c + 1)].partition_broadcast(64),
                )

        def load_esca(a):
            rows = err_scales.rearrange("g (k r) n -> r k g n", r=4)
            for r in range(4):
                nc.sync.dma_start(out=esca[a][r:P:32, :, :].bitcast(I32), in_=rows[r, :, 2 * a : 2 * a + 2, :].bitcast(I32))

        def load_ewor(g):
            nc.sync.dma_start(out=ewor[g][:].bitcast(I32), in_=err_words[g].bitcast(I32))

        xgrp = {}
        xord = {}

        def xsort(g, lo, hi, eng):
            xo = work.tile([P, (hi - lo) * 512], F32, name="xo", tag="xo", bufs=4)
            copy_on(
                eng,
                xo[:].rearrange("p (a u m) -> p a m u", u=2, m=P),
                xrun[g, lo, hi].bitcast(F32).rearrange("p (a m u) -> p a m u", u=2, m=P),
            )
            for t in range(lo, hi):
                xord[g, t] = xo[:, 512 * (t - lo) : 512 * (t - lo + 1)]

        def trans(g, t, passes=range(Q)):
            if passes[0] == 0:
                xbank[g, t] = take(("x", g, t), [P, 512])
            b = xbank[g, t]
            words = xraw[g, t].bitcast(F32)
            for q in passes:
                for u in range(2):
                    j = 2 * q + u
                    if (g, t) in xord:
                        cols = xord[g, t][:, P * j : P * (j + 1)]
                    else:
                        cols = words[:, 256 * q + u : 256 * (q + 1) : 2]
                    nc.tensor.transpose(b[:, P * j : P * (j + 1)], cols, ident[:])

        xbank = {}

        def xevict(g, t, eng, passes=range(Q)):
            if (g, t // 2) not in xgrp:
                xgrp[g, t // 2] = work.tile([P, 2 * D], BF16, name="xg", tag="xg", bufs=3, align_bytes=64)
            lo, hi = passes[0], passes[-1] + 1
            dst = xgrp[g, t // 2][:, D * (t % 2) + 512 * lo : D * (t % 2) + 512 * hi]
            copy_on(
                eng,
                dst.bitcast(F32).rearrange("p (q m u) -> p q m u", m=P, u=2),
                xbank[g, t][:, 256 * lo : 256 * hi].rearrange("p (q u m) -> p q m u", m=P, u=2),
            )
            if hi == Q:
                give(("x", g, t))

        def xquant(g, lo, hi):
            first = 2 * Q * (lo // (2 * Q))
            nc.vector.quantize_mx(
                out=xcod[g][:, P * lo : P * hi].bitcast(FP8X4),
                scales=xsca[g][:, P * lo : P * hi],
                in_=xgrp[g, lo // (2 * Q)][:, 512 * (lo - first) : 512 * (hi - first)],
            )

        wgrp = {}

        def winter(c, q, eng, lo=0, hi=WC):
            if c not in wgrp:
                wgrp[c] = work.tile([P, Q * WC * 4], BF16, name="wg", tag="wg", bufs=2, align_bytes=64)
            copy_on(
                eng,
                wgrp[c][:, 4 * (WC * q + lo) : 4 * (WC * q + hi)].rearrange("p (c i j) -> p c j i", i=4, j=4),
                wraw[c][q][:, :, lo:hi].rearrange("p j (c i) -> p c j i", i=4),
            )

        def wquant(c, lo, hi):
            nc.vector.quantize_mx(
                out=wcod[c][:, WC * lo : WC * hi].bitcast(FP8X4),
                scales=wsca[c][:, WC * lo : WC * hi],
                in_=wgrp[c][:, 4 * WC * lo : 4 * WC * hi],
            )

        abank = {}

        def lhuc_turn():
            abank["turn"] = take("turn", [P, P])
            nc.tensor.transpose(abank["turn"][:], lrow[:].bitcast(F32), ident[:])

        def lhuc_keep():
            nc.vector.tensor_copy(out=lcol[:].rearrange("p s c -> p (s c)"), in_=abank["turn"][:, 0 : SPK * NC])

        def lhuc_repeat(c, lo, hi, cols):
            nc.vector.tensor_copy(
                out=lrep[c][:, 2 * lo : 2 * hi, :],
                in_=cols[:, 2 * lo : 2 * hi, c : c + 1].to_broadcast([P, 2 * (hi - lo), 64]),
            )

        def lhuc_spread(c, lo, hi):
            abank[c, lo] = take(("amp", c, lo), [P, (hi - lo) * P])
            for g in range(lo, hi):
                cols = lrep[c][:, 2 * g : 2 * g + 2, :].rearrange("p s r -> p (s r)")
                nc.tensor.transpose(abank[c, lo][:, P * (g - lo) : P * (g - lo + 1)], cols, ident[:])

        def lhuc_park(c):
            nc.scalar.copy(out=lraw[c - 1][:].rearrange("p g n -> p (g n)").bitcast(F32), in_=abank[c, 0][:])
            give(("amp", c, 0))

        def sigm(c, lo, hi):
            dst = amp[c][:, lo:hi, :].rearrange("p g n -> p (g n)")
            if c == 0:
                nc.scalar.activation(out=dst, in_=abank[c, lo][:].bitcast(BF16), func=ACT.Sigmoid)
                give(("amp", c, lo))
            else:
                nc.scalar.activation(out=dst, in_=lraw[c - 1][:, lo:hi, :].rearrange("p g n -> p (g n)"), func=ACT.Sigmoid)

        halves = {}
        zb = {}
        hgrp = {}

        def s1(g, c, u, passes=range(Q)):
            if passes[0] == 0:
                if u == 0:
                    halves[g, c] = work.tile([P, 2, WC, 2], BF16, name="half", tag="half", bufs=3, align_bytes=64)
                zb[g, c, u] = take(("z", g, c, u), [P, 2, WC])
            for e in range(2):
                for q in passes:
                    t = 2 * u + e
                    nc.tensor.matmul_mx(
                        out=zb[g, c, u][:, e, :],
                        lhsT=xcod[g][:, P * (Q * t + q) : P * (Q * t + q + 1)].bitcast(FP8X4),
                        lhsT_scale=xsca[g][:, P * (Q * t + q) : P * (Q * t + q + 1)],
                        rhs=wcod[c][:, WC * q : WC * (q + 1)].bitcast(FP8X4),
                        rhs_scale=wsca[c][:, WC * q : WC * (q + 1)],
                        start=(q == 0 and e == 0),
                        stop=(q == Q - 1 and e == 1),
                    )

        def hevict(g, c, u):
            nc.vector.scalar_tensor_tensor(
                out=halves[g, c][:, u, :, :],
                in0=zb[g, c, u][:].rearrange("p e n -> p n e"),
                scalar=0.0,
                in1=amp[c][:, g, :].unsqueeze(2).to_broadcast([P, WC, 2]),
                op0=ALU.max,
                op1=ALU.mult,
            )
            give(("z", g, c, u))

        def hjoin(g, c, eng):
            hg = work.tile([P, WC * 4], BF16, name="hg", tag="hg", bufs=3, align_bytes=64)
            copy_on(
                eng,
                hg[:].bitcast(F32).rearrange("p (n u) -> p n u", u=2),
                halves[g, c][:].rearrange("p u n e -> p (u n e)").bitcast(F32).rearrange("p (u n) -> p n u", u=2),
            )
            hgrp[g, c] = hg

        def hquant(g, c):
            nc.vector.quantize_mx(out=hcod[c][:, g, :].bitcast(FP8X4), scales=hsca[c][:, g, :], in_=hgrp.pop((g, c))[:])

        ob = {}
        og = {}

        def s2(h, lo, hi, groups):
            if groups[0] == 0:
                ob[h, lo] = take(("o", h, lo), [P, hi - lo])
            for g in groups:
                nc.tensor.matmul_mx(
                    out=ob[h, lo][:],
                    lhsT=hcod[h // 2][:, g, P * (h % 2) : P * (h % 2 + 1)].bitcast(FP8X4),
                    lhsT_scale=hsca[h // 2][:, g, P * (h % 2) : P * (h % 2 + 1)],
                    rhs=ewor[g][:, 2 * lo : 2 * hi].bitcast(FP4X4),
                    rhs_scale=esca[g // 2][:, g % 2, lo:hi],
                    start=(g == 0),
                    stop=(g == G - 1),
                )

        def oevict(h, lo, hi, eng):
            if h not in og:
                og[h] = work.tile([P, S], F32, name="og", tag="og", bufs=3, align_bytes=256)
            dst = og[h][:, lo:hi]
            if eng == "s":
                nc.scalar.activation(out=dst, in_=ob[h, lo][:], func=ACT.Copy, scale=2.0)
            else:
                nc.vector.tensor_scalar(out=dst, in0=ob[h, lo][:], scalar1=2.0, scalar2=None, op0=ALU.mult)
            give(("o", h, lo))

        def store(h, lo, hi):
            nc.sync.dma_start(out=out[P * h : P * (h + 1), lo:hi], in_=og[h][:, lo:hi])

        with tc.manual_schedule():
            nc.sync.dma_start(out=lrow[0:32, :], in_=lhuc.rearrange("s (c n) -> (s c) n", n=WC))
            nc.vector.memset(lrow[32:64, :], 0.0)
            nc.vector.memset(lrow[64:128, :], 0.0)
            make_identity(nc, ident[:])
            for plane in esca:
                nc.vector.memset(plane[:].rearrange("p g n -> p (g n)").bitcast(I32), 0)
            load_x(0, 0, 1)
            load_w(0, [0])
            load_x(0, 1, 2)
            load_w(0, [1])
            load_x(0, 2, 3)
            load_x(0, 3, 4)
            load_x(1, 0, 1)
            load_x(1, 1, 2)
            load_x(1, 2, 4)
            load_x(2, 0, 2)
            load_x(2, 2, 4)
            load_x(3, 0, 3)
            load_x(3, 3, 4)
            load_esca(0)
            load_esca(1)
            load_ewor(0)
            load_w(1)
            load_ewor(1)
            load_ewor(2)
            load_ewor(3)
            load_w(2)
            load_lhuc_spread(2)
            load_w(3)
            load_lhuc_spread(3)

            def stage(k, c):
                g, u = divmod(k, 2)
                s1(g, c, u)
                hevict(g, c, u)
                if u == 1:
                    hjoin(g, c, "s")
                    if (g - 1, c) in hgrp:
                        hquant(g - 1, c)

            def finish(h, n):
                oevict(h, 512 * n, 512 * (n + 1), "s")
                store(h, 512 * n, 512 * (n + 1))

            def s2row(h, g, banks):
                for n in banks:
                    s2(h, 512 * n, 512 * (n + 1), [g])

            def turn(g, lo, hi):
                for t in range(lo, hi):
                    trans(g, t)
                    xevict(g, t, "s")

            def half(g, c, u):
                s1(g, c, u)
                hevict(g, c, u)

            lhuc_turn()
            lhuc_keep()
            lhuc_repeat(0, 0, 1, abank["turn"][:, 0 : SPK * NC].rearrange("p (s c) -> p s c", c=NC))
            give("turn")
            lhuc_repeat(0, 1, G, lcol)
            trans(0, 0, [0])
            lhuc_spread(0, 0, 1)
            trans(0, 0, [1])
            sigm(0, 0, 1)
            xevict(0, 0, "s")
            lhuc_spread(0, 1, G)
            trans(0, 1)
            xevict(0, 1, "s")
            winter(0, 0, "v")
            lhuc_repeat(1, 0, G, lcol)
            lhuc_spread(1, 0, G)
            lhuc_park(1)
            wquant(0, 0, 1)
            winter(0, 1, "v")
            xquant(0, 0, 2)
            wquant(0, 1, 2)
            xquant(0, 2, 4)
            turn(0, 2, 3)
            s1(0, 0, 0)

            sigm(0, 1, G)
            xsort(1, 0, 1, "v")
            xsort(1, 1, 2, "v")
            xquant(0, 4, 6)
            trans(0, 3)
            xevict(0, 3, "s", [0])
            xevict(0, 3, "s", [1])
            hevict(0, 0, 0)
            xsort(1, 3, 4, "v")
            xquant(0, 6, 7)
            xquant(0, 7, 8)
            turn(1, 0, 3)
            s1(0, 0, 1)
            xsort(2, 0, 1, "v")
            xquant(1, 0, 4)
            turn(1, 3, 4)
            turn(2, 0, 2)
            xsort(2, 2, 4, "v")
            s1(1, 0, 0)
            xquant(1, 4, 8)
            xquant(2, 0, 2)
            hevict(0, 0, 1)
            turn(2, 2, 4)
            hjoin(0, 0, "s")
            xquant(2, 2, 4)
            s1(1, 0, 1)
            s1(2, 0, 0)
            xsort(3, 0, 1, "v")
            xsort(3, 1, 2, "v")
            xquant(2, 4, 8)
            hquant(0, 0)
            for t in range(4):
                trans(3, t)
            s1(2, 0, 1)
            xevict(3, 0, "s")
            hevict(1, 0, 0)
            xevict(3, 1, "s")
            hevict(1, 0, 1)
            xevict(3, 2, "s")
            xevict(3, 3, "s")
            hjoin(1, 0, "s")
            xquant(3, 0, 4)
            s2row(0, 0, [0, 1, 2])
            s2row(1, 0, [0, 1])
            s1(3, 0, 0)
            hevict(2, 0, 0)
            xquant(3, 4, 8)
            hquant(1, 0)
            s1(3, 0, 1)
            winter(1, 0, "s")
            winter(1, 1, "s")
            hevict(2, 0, 1)
            hjoin(2, 0, "s")
            hevict(3, 0, 0)
            wquant(1, 0, 1)
            wquant(1, 1, 2)
            hevict(3, 0, 1)
            sigm(1, 0, 1)
            hjoin(3, 0, "s")
            s2row(0, 1, [0, 1, 2])
            s2row(1, 1, [0, 1])
            s2row(1, 0, [2])
            s2row(1, 1, [2])
            sigm(1, 1, G)
            hquant(2, 0)
            s1(0, 1, 0)
            hevict(0, 1, 0)
            hquant(3, 0)

            s1(0, 1, 1)
            hevict(0, 1, 1)
            hjoin(0, 1, "s")
            s2row(0, 2, [0, 1, 2])
            half(1, 1, 0)
            winter(2, 0, "v")
            s2row(1, 2, [0, 1])
            half(1, 1, 1)
            s2row(0, 3, [0])
            finish(0, 0)
            s2row(0, 3, [1])
            finish(0, 1)
            hquant(0, 1)
            hjoin(1, 1, "s")
            s2row(0, 3, [2])
            finish(0, 2)
            s2row(1, 3, [0])
            finish(1, 0)
            half(2, 1, 0)
            winter(2, 1, "v")
            s2row(1, 3, [1])
            finish(1, 1)
            half(2, 1, 1)
            hquant(1, 1)
            hjoin(2, 1, "s")
            s2row(1, 2, [2])
            s2row(1, 3, [2])
            finish(1, 2)
            sigm(2, 0, 2)
            wquant(2, 0, 2)
            half(3, 1, 0)
            s2row(2, 0, [0, 1])
            half(3, 1, 1)
            hquant(2, 1)
            hjoin(3, 1, "s")
            s2row(2, 0, [2])
            s2row(3, 0, [0])
            s2row(2, 1, [0])
            sigm(2, 2, G)
            half(0, 2, 0)
            hquant(3, 1)
            s2row(2, 1, [1])
            half(0, 2, 1)
            hjoin(0, 2, "s")
            winter(3, 1, "s")
            s2row(2, 1, [2])
            s2row(3, 1, [0])
            half(1, 2, 0)
            winter(3, 0, "v")
            hquant(0, 2)
            s2row(2, 2, [0, 1])
            half(1, 2, 1)
            hjoin(1, 2, "s")
            sigm(3, 0, 2)
            s2row(2, 2, [2])
            s2row(3, 2, [0])
            half(2, 2, 0)
            hquant(1, 2)
            for n in range(2):
                s2row(2, 3, [n])
                finish(2, n)
            half(2, 2, 1)
            hjoin(2, 2, "s")
            wquant(3, 0, 2)
            s2row(2, 3, [2])
            finish(2, 2)
            s2row(3, 3, [0])
            finish(3, 0)
            half(3, 2, 0)
            hquant(2, 2)
            s2(3, 512, 1024, [0, 1])
            half(3, 2, 1)
            hjoin(3, 2, "v")
            s2(3, 512, 1024, [2, 3])
            finish(3, 1)
            hquant(3, 2)
            s2(3, 1024, S, range(G))
            finish(3, 2)
            sigm(3, 2, G)
            for i in range(2 * NS):
                h, n = 4 + i // NS, i % NS
                if i < G:
                    half(i, 3, 0)
                    if i > 0:
                        hquant(i - 1, 3)
                    half(i, 3, 1)
                    hjoin(i, 3, "s")
                if i == G:
                    hquant(G - 1, 3)
                if i == 0:
                    s2(h, 0, 512, range(G - 1))
                    continue
                if i == 1:
                    s2(h, 0, 512, [G - 1])
                    finish(h, 0)
                s2(h, 512 * n, 512 * (n + 1), range(G))
                finish(h, n)
            for n in range(NS):
                s2(NH - 2, 512 * n, 512 * (n + 1), range(G))
                finish(NH - 2, n)
            cuts = [0, 512, 768, 1024, 1280, 1408, S]
            for i in range(len(cuts) - 1):
                s2(NH - 1, cuts[i], cuts[i + 1], range(G))
                oevict(NH - 1, cuts[i], cuts[i + 1], "sv"[i % 2])
                store(NH - 1, cuts[i], cuts[i + 1])
